import numpy as np
import ml_dtypes


def mxq(x, axis, fmt="e4m3"):
    dtype, down = {"e4m3": (ml_dtypes.float8_e4m3fn, 7), "e5m2": (ml_dtypes.float8_e5m2, 14)}[fmt]
    v = np.moveaxis(np.asarray(x, np.float32).astype(ml_dtypes.bfloat16).astype(np.float64), axis, -1)
    blocks = v.reshape(v.shape[:-1] + (-1, 32))
    amax = np.abs(blocks).max(-1, keepdims=True)
    byte = np.maximum(np.where(amax > 0, np.frexp(amax)[1] - 1 + 127, 0) - down, 1)
    scale = np.exp2(byte - 127.0)
    codes = (blocks / scale).astype(np.float32).astype(dtype).astype(np.float64)
    return np.moveaxis((codes * scale).reshape(v.shape), -1, axis)


WIDE = False


def mx_kscale(k):
    if not WIDE:
        return np.ones(k)
    levels = np.array([10, -10, 5, -5, 0])
    if k % 512:
        return np.exp2(np.random.permutation(np.resize(levels, k // 32))).repeat(32)
    a = np.empty((k // 512, 16))
    for p in range(k // 512):
        a[p, :8] = np.random.permutation(np.resize(levels, 8))
        for g in range(8):
            far = levels[np.abs(levels - a[p, g]) >= 10]
            a[p, g + 8] = far[np.random.randint(len(far))]
    return np.exp2(a.ravel()).repeat(32)


BF16 = ml_dtypes.bfloat16


def bf(x):
    return np.asarray(x, np.float32).astype(BF16)


def f64(x):
    return np.asarray(x).astype(np.float64)


E2M1 = np.array([0.0, 0.5, 1.0, 1.5, 2.0, 3.0, 4.0, 6.0, -0.0, -0.5, -1.0, -1.5, -2.0, -3.0, -4.0, -6.0])


def pack_weight(w, fmt):
    k, n = w.shape
    w = f64(bf(w)).reshape(k // 32, 32, n)
    amax = np.abs(w).max(1)
    if fmt == "e4m3":
        byte = np.frexp(amax)[1] - 1 + 127 - 7
    else:
        mant, ex = np.frexp(amax / 6.0)
        byte = np.where(mant > 0.5, ex, ex - 1) + 127
    byte = np.clip(np.where(amax > 0, byte, 1), 1, 254)
    scaled = (w * np.exp2(127.0 - byte)[:, None, :]).reshape(k, n).astype(np.float32)
    by_word = np.ascontiguousarray(scaled.reshape(k // 512, 128, 4, n).transpose(0, 1, 3, 2))
    if fmt == "e4m3":
        words = by_word.astype(ml_dtypes.float8_e4m3fn).view(np.uint8)
    else:
        c = by_word.astype(ml_dtypes.float4_e2m1fn).view(np.uint8) & 0xF
        words = c[..., 0::2] | (c[..., 1::2] << 4)
    return np.ascontiguousarray(words), np.ascontiguousarray(byte.astype(np.uint8).reshape(k // 512, 16, n))


def unpack_weight(words, scales, fmt):
    g, p, n, _ = words.shape
    if fmt == "e4m3":
        vals = np.ascontiguousarray(words).view(ml_dtypes.float8_e4m3fn).astype(np.float64)
    else:
        nib = np.empty((g, p, n, 4), np.uint8)
        nib[..., 0::2] = words & 0xF
        nib[..., 1::2] = words >> 4
        vals = E2M1[nib]
    vals = vals * np.repeat(np.exp2(scales.astype(np.float64) - 127.0), 8, axis=1)[..., None]
    return vals.transpose(0, 1, 3, 2).reshape(g * 512, n)
def pack4(w):
    words, scales = pack_weight(w, "e2m1")
    return words.reshape(words.shape[0], 128, -1), scales


def unpack4(words, scales):
    return unpack_weight(words.reshape(words.shape[0], 128, -1, 2), scales, "e2m1")


def planes(Y):
    n, m = Y.shape
    b = f64(bf(Y)).reshape(n // 32, 32, m)
    amax = np.abs(b).max(1)
    byte = np.clip(np.where(amax > 0, np.frexp(amax)[1] - 1 + 127 - 7, 1), 1, 254)
    codes = (b * np.exp2(127.0 - byte)[:, None, :]).reshape(n, m).astype(np.float32).astype(ml_dtypes.float8_e4m3fn).view(np.uint8)
    words = codes.reshape(n // 512, 128, 4, m).transpose(0, 1, 3, 2)
    return np.ascontiguousarray(words), np.ascontiguousarray(byte.astype(np.uint8).reshape(n // 512, 16, m))


CLIPS, T, K, BINS = 4, 512, 1024, 1536

ROWS = CLIPS * T


def cosine_basis(phase):
    u = np.arange(K)[:, None]
    omega = np.pi * (np.arange(BINS) + 0.5)[None, :] / BINS
    return np.sqrt(2.0 / K) * np.cos(omega * u + phase[None, :])


def setup_inputs():
    s = mx_kscale(K)
    frames = np.random.randn(CLIPS, T, K) * s
    phase = np.random.uniform(0.0, 2.0 * np.pi, BINS)
    basis_words, basis_scales = pack4(cosine_basis(phase) / s[:, None])
    eq = np.exp(0.4 * np.random.randn(BINS))
    frame_gain = np.exp(0.3 * np.random.randn(CLIPS, T))
    base_power = 0.25 * np.exp(0.5 * np.random.randn(BINS))
    return {"frames": bf(frames), "basis_words": basis_words, "basis_scales": basis_scales,
            "eq": bf(eq), "frame_gain": bf(frame_gain), "base_power": bf(base_power)}


def reference(frames, basis_words, basis_scales, eq, frame_gain, base_power):
    x = f64(frames).reshape(ROWS, K)
    C = unpack4(basis_words, basis_scales)
    amp = mxq(x, 1, "e4m3") @ C
    a = amp * f64(eq)[None, :]
    power = a * a * f64(frame_gain).reshape(ROWS, 1) + f64(base_power)[None, :]
    y = power.reshape(CLIPS, T, BINS)
    Y = y.reshape(ROWS, BINS).T
    words, scales = planes(Y)
    return y, words, scales

@@ -1,0 +1,255 @@
+from contextlib import ExitStack
+
+import concourse.mybir as mybir
+from concourse.masks import make_identity
+
+CLIPS, T, K, BINS = 4, 512, 1024, 1536
+FLOPS = 2 * CLIPS * T * K * BINS
+
+F32 = mybir.dt.float32
+BF16 = mybir.dt.bfloat16
+I32 = mybir.dt.int32
+U32 = mybir.dt.uint32
+U8 = mybir.dt.uint8
+FP8X4 = mybir.dt.float8_e4m3fn_x4
+FP4X4 = mybir.dt.float4_e2m1fn_x4
+ALU = mybir.AluOpType
+ACT = mybir.ActivationFunctionType
+
+P = 128
+BANK = 512
+BANKS = 8
+K_PASSES = K // 512
+GROUPS = BINS // 512
+UNITS = CLIPS * GROUPS
+GAIN_ROWS = CLIPS * T // P
+EQ_ROWS = BINS // P
+PLANE_LAG = 2
+
+
+def tile_cosine_power_for_mel_g4_kernel(
+    tc, frames, basis_words, basis_scales, eq, frame_gain, base_power, out_0, out_1, out_2
+):
+    nc = tc.nc
+    with ExitStack() as ctx:
+        keep = ctx.enter_context(tc.tile_pool(name="keep", bufs=1))
+        work = ctx.enter_context(tc.tile_pool(name="work", bufs=2))
+        psum = ctx.enter_context(tc.psum_pool(name="psum", bufs=1))
+        ctx.enter_context(tc.manual_schedule())
+
+        bank_count = [0]
+
+        def next_bank():
+            tag = "bank%d" % (bank_count[0] % BANKS)
+            bank_count[0] = bank_count[0] + 1
+            return psum.tile([P, BANK], F32, name=tag, tag=tag)
+
+        frame_words = frames.bitcast(F32)
+        x_raw = {}
+
+        def load_frames(c, h):
+            raw = work.tile([P, 2, K // 2], F32, name="x_raw", tag="x_raw", bufs=2 * CLIPS)
+            rows = frame_words[c, 2 * P * h : 2 * P * (h + 1), :]
+            nc.sync.dma_start(out=raw[:], in_=rows.rearrange("(j p) w -> p j w", p=P))
+            x_raw[(c, h)] = raw
+
+        ident = keep.tile([P, P], F32)
+        make_identity(nc, ident[:])
+        rows_f32 = keep.tile([P, P], F32)
+        nc.gpsimd.memset(rows_f32[:], 0.0)
+        c_scales = keep.tile([P, K_PASSES, BINS], U8, align_bytes=64)
+        nc.vector.memset(c_scales[:].rearrange("p g n -> p (g n)").bitcast(I32), 0)
+
+        load_frames(0, 0)
+        load_frames(0, 1)
+        rows_bf = keep.tile([P, P], BF16)
+        nc.sync.dma_start(
+            out=rows_bf[0:GAIN_ROWS, :], in_=frame_gain.rearrange("c (j p) -> (c j) p", p=P)
+        )
+        nc.sync.dma_start(
+            out=rows_bf[GAIN_ROWS : GAIN_ROWS + EQ_ROWS, :], in_=eq.rearrange("(b p) -> b p", p=P)
+        )
+        for q in range(4):
+            nc.sync.dma_start(
+                out=c_scales[32 * q : 32 * q + 4, :, :].bitcast(I32),
+                in_=basis_scales[:, 4 * q : 4 * q + 4, :].rearrange("g r n -> r g n").bitcast(I32),
+            )
+        c_words = keep.tile([P, K_PASSES, 2 * BINS], U8, align_bytes=64)
+        nc.sync.dma_start(
+            out=c_words[:].bitcast(I32), in_=basis_words.rearrange("g p n -> p g n").bitcast(I32)
+        )
+        base_rows = keep.tile([P, BINS], BF16)
+        nc.sync.dma_start(out=base_rows[:], in_=base_power.partition_broadcast(P))
+        for c in range(1, CLIPS):
+            load_frames(c, 0)
+            load_frames(c, 1)
+
+        def copy_out(engine, out, bank):
+            src = bank[:].rearrange("p (j u m) -> p j m u", j=2, u=2)
+            dst = out.rearrange("p (j m u) -> p j m u", j=2, u=2)
+            if engine == "scalar":
+                nc.scalar.copy(out=dst, in_=src)
+            else:
+                nc.vector.tensor_copy(out=dst, in_=src)
+
+        x_turned, x_codes, x_scales = {}, {}, {}
+
+        def turn_frames(c, g, h, engine):
+            if h == 0:
+                x_turned[(c, g)] = work.tile(
+                    [P, 2 * T], F32, name="x_turned", tag="x_turned", bufs=3, align_bytes=64
+                )
+            bank = next_bank()
+            for j in range(2):
+                for u in range(2):
+                    nc.tensor.transpose(
+                        bank[:, P * (2 * j + u) : P * (2 * j + u + 1)],
+                        x_raw[(c, h)][:, j, 256 * g + u : 256 * (g + 1) : 2],
+                        ident[:],
+                    )
+            copy_out(engine, x_turned[(c, g)][:, BANK * h : BANK * (h + 1)], bank)
+
+        def quantize_frames(c, g):
+            codes = work.tile([P, T], U32, name="x_codes", tag="x_codes", bufs=4, align_bytes=64)
+            scales = work.tile([P, T], U8, name="x_scales", tag="x_scales", bufs=4, align_bytes=64)
+            nc.vector.quantize_mx(
+                out=codes[:].bitcast(FP8X4), scales=scales[:], in_=x_turned[(c, g)][:].bitcast(BF16)
+            )
+            x_codes[(c, g)], x_scales[(c, g)] = codes, scales
+
+        used = GAIN_ROWS + EQ_ROWS
+        turn_frames(0, 0, 0, "scalar")
+        turn_frames(0, 0, 1, "vector")
+        turn_frames(0, 1, 0, "scalar")
+        quantize_frames(0, 0)
+        nc.vector.tensor_copy(out=rows_f32[0:used, :], in_=rows_bf[0:used, :])
+        turn_frames(0, 1, 1, "scalar")
+        cols = keep.tile([P, used], F32)
+        bank = next_bank()
+        nc.tensor.transpose(bank[:, 0:P], rows_f32[:], ident[:])
+        nc.vector.tensor_copy(out=cols[:], in_=bank[:, 0:used])
+        quantize_frames(0, 1)
+
+        squares, y_rows, y_pairs, y_turned, planes = {}, {}, {}, {}, {}
+
+        def multiply(s):
+            c, grp = divmod(s, GROUPS)
+            for b in range(4):
+                blk = 4 * grp + b
+                bank = next_bank()
+                for g in range(K_PASSES):
+                    nc.tensor.matmul_mx(
+                        out=bank[:],
+                        lhsT=c_words[:, g, 2 * P * blk : 2 * P * (blk + 1)].bitcast(FP4X4),
+                        lhsT_scale=c_scales[:, g, P * blk : P * (blk + 1)],
+                        rhs=x_codes[(c, g)][:].bitcast(FP8X4),
+                        rhs_scale=x_scales[(c, g)][:],
+                        start=(g == 0),
+                        stop=(g == K_PASSES - 1),
+                    )
+                sq = work.tile([P, T], F32, name="squares", tag="squares", bufs=8)
+                nc.scalar.activation(
+                    out=sq[:],
+                    in_=bank[:],
+                    func=ACT.Square,
+                    scale=cols[:, GAIN_ROWS + blk : GAIN_ROWS + blk + 1],
+                )
+                squares[(s, b)] = sq
+
+        def power(s):
+            c, grp = divmod(s, GROUPS)
+            for h in range(2):
+                y = work.tile([P, 2, BANK], F32, name="y_rows", tag="y_rows", bufs=6)
+                for j in range(2):
+                    tile_no = 2 * h + j
+                    bank = next_bank()
+                    for b in range(4):
+                        nc.tensor.transpose(
+                            bank[:, P * b : P * (b + 1)],
+                            squares[(s, b)][:, P * tile_no : P * (tile_no + 1)],
+                            ident[:],
+                        )
+                    nc.vector.scalar_tensor_tensor(
+                        out=y[:, j, :],
+                        in0=bank[:],
+                        scalar=cols[:, 4 * c + tile_no : 4 * c + tile_no + 1],
+                        in1=base_rows[:, BANK * grp : BANK * (grp + 1)],
+                        op0=ALU.mult,
+                        op1=ALU.add,
+                    )
+                dst = out_0[c, 2 * P * h : 2 * P * (h + 1), BANK * grp : BANK * (grp + 1)]
+                nc.sync.dma_start(out=dst.rearrange("(j p) n -> p j n", p=P), in_=y[:])
+                y_rows[(s, h)] = y
+
+        def round_pairs(s, h):
+            pairs = work.tile([P, 2 * BANK], BF16, name="y_pairs", tag="y_pairs", bufs=6)
+            nc.vector.tensor_copy(
+                out=pairs[:].rearrange("p (j u q e) -> p j u q e", j=2, u=2, e=2),
+                in_=y_rows[(s, h)][:].rearrange("p j (q u e) -> p j u q e", u=2, e=2),
+            )
+            y_pairs[(s, h)] = pairs
+
+        def turn_pairs(s, h, engine):
+            if h == 0:
+                y_turned[s] = work.tile(
+                    [P, 2 * T], F32, name="y_turned", tag="y_turned", bufs=3, align_bytes=64
+                )
+            bank = next_bank()
+            words = y_pairs[(s, h)][:].bitcast(F32)
+            for i in range(4):
+                nc.tensor.transpose(
+                    bank[:, P * i : P * (i + 1)], words[:, P * i : P * (i + 1)], ident[:]
+                )
+            copy_out(engine, y_turned[s][:, BANK * h : BANK * (h + 1)], bank)
+
+        def quantize_power(s):
+            c, grp = divmod(s, GROUPS)
+            if grp == 0:
+                planes[c] = work.tile(
+                    [P, GROUPS, T], U8, name="y_scales", tag="y_scales", bufs=2, align_bytes=64
+                )
+            codes = work.tile([P, T], U32, name="y_codes", tag="y_codes", bufs=3, align_bytes=64)
+            nc.vector.quantize_mx(
+                out=codes[:].bitcast(FP8X4),
+                scales=planes[c][:, grp, :],
+                in_=y_turned[s][:].bitcast(BF16),
+            )
+            dst = out_1[grp, :, T * c : T * (c + 1), :].rearrange("p m t -> p (m t)")
+            nc.sync.dma_start(out=dst.bitcast(I32), in_=codes[:].bitcast(I32))
+            if grp == GROUPS - 1:
+                for q in range(4):
+                    rows = out_2[:, 4 * q : 4 * q + 4, T * c : T * (c + 1)]
+                    nc.sync.dma_start(
+                        out=rows.rearrange("g r m -> r g m").bitcast(I32),
+                        in_=planes[c][32 * q : 32 * q + 4, :, :].bitcast(I32),
+                    )
+
+        for s in range(UNITS):
+            c, grp = divmod(s, GROUPS)
+            feeds_next = c + 1 < CLIPS and grp < K_PASSES
+            multiply(s)
+            if feeds_next:
+                turn_frames(c + 1, grp, 0, "scalar")
+                turn_frames(c + 1, grp, 1, "scalar")
+            if s >= PLANE_LAG:
+                turn_pairs(s - PLANE_LAG, 0, "scalar")
+                turn_pairs(s - PLANE_LAG, 1, "scalar")
+            if s == UNITS - 1:
+                turn_pairs(s - 1, 0, "scalar")
+                turn_pairs(s - 1, 1, "scalar")
+            power(s)
+            if s == UNITS - 1:
+                round_pairs(s, 0)
+                round_pairs(s, 1)
+                turn_pairs(s, 0, "scalar")
+                turn_pairs(s, 1, "scalar")
+                quantize_power(s - 2)
+                quantize_power(s - 1)
+                quantize_power(s)
+            else:
+                if s >= PLANE_LAG:
+                    quantize_power(s - PLANE_LAG)
+                round_pairs(s, 0)
+                round_pairs(s, 1)
+                if feeds_next:
+                    quantize_frames(c + 1, grp)

@@ -24,7 +24,18 @@ GROUPS = BINS // 512
 UNITS = CLIPS * GROUPS
 GAIN_ROWS = CLIPS * T // P
 EQ_ROWS = BINS // P
-PLANE_LAG = 2
+CAST = (("scalar", "scalar"), ("vector", "vector"), ("vector", "vector"))
+TOK = (0,)
+SORT0 = 1
+SCAST = (2,)
+R0 = ("vector", "vector")
+ORDER = "x00 x01 x02 x03 w0 s e r w1 x10 x11 x12 x13 b w2"
+UNSORT = 16
+SQ0 = 2
+SC = (2, 5, 8, 9, 10)
+T9 = "scalar"
+T11 = "scalar"
+FEED0 = 0
 
 
 def tile_cosine_power_for_mel_g4_kernel(
@@ -47,176 +58,290 @@ def tile_cosine_power_for_mel_g4_kernel(
         frame_words = frames.bitcast(F32)
         x_raw = {}
 
-        def load_frames(c, h):
-            raw = work.tile([P, 2, K // 2], F32, name="x_raw", tag="x_raw", bufs=2 * CLIPS)
-            rows = frame_words[c, 2 * P * h : 2 * P * (h + 1), :]
-            nc.sync.dma_start(out=raw[:], in_=rows.rearrange("(j p) w -> p j w", p=P))
-            x_raw[(c, h)] = raw
+        def load_frames(c, j):
+            raw = work.tile([P, K // 2], F32, name="x_raw", tag="x_raw", bufs=4 * CLIPS)
+            nc.sync.dma_start(out=raw[:], in_=frame_words[c, P * j : P * (j + 1), :])
+            x_raw[(c, j)] = raw
+
+        c_words = {}
+
+        def load_basis(grp):
+            words = keep.tile(
+                [P, K_PASSES, 2 * BANK], U8, name="c_words%d" % grp, align_bytes=64
+            )
+            src = basis_words[:, :, 2 * BANK * grp : 2 * BANK * (grp + 1)]
+            nc.sync.dma_start(
+                out=words[:].bitcast(I32), in_=src.rearrange("g p n -> p g n").bitcast(I32)
+            )
+            c_words[grp] = words
 
         ident = keep.tile([P, P], F32)
         make_identity(nc, ident[:])
         rows_f32 = keep.tile([P, P], F32)
-        nc.gpsimd.memset(rows_f32[:], 0.0)
         c_scales = keep.tile([P, K_PASSES, BINS], U8, align_bytes=64)
         nc.vector.memset(c_scales[:].rearrange("p g n -> p (g n)").bitcast(I32), 0)
+        nc.vector.memset(rows_f32[:], 0.0)
 
-        load_frames(0, 0)
-        load_frames(0, 1)
+        base_rows = {}
+
+        def load_base(first, last):
+            rows = keep.tile([P, last - first], BF16, name="base_rows%d" % first)
+            nc.sync.dma_start(out=rows[:], in_=base_power[first:last].partition_broadcast(P))
+            for grp in range(first // BANK, last // BANK):
+                base_rows[grp] = rows[:, BANK * grp - first : BANK * (grp + 1) - first]
+
+        eq_rows = keep.tile([P, BANK], BF16)
         rows_bf = keep.tile([P, P], BF16)
-        nc.sync.dma_start(
-            out=rows_bf[0:GAIN_ROWS, :], in_=frame_gain.rearrange("c (j p) -> (c j) p", p=P)
-        )
-        nc.sync.dma_start(
-            out=rows_bf[GAIN_ROWS : GAIN_ROWS + EQ_ROWS, :], in_=eq.rearrange("(b p) -> b p", p=P)
-        )
-        for q in range(4):
-            nc.sync.dma_start(
-                out=c_scales[32 * q : 32 * q + 4, :, :].bitcast(I32),
-                in_=basis_scales[:, 4 * q : 4 * q + 4, :].rearrange("g r n -> r g n").bitcast(I32),
-            )
-        c_words = keep.tile([P, K_PASSES, 2 * BINS], U8, align_bytes=64)
-        nc.sync.dma_start(
-            out=c_words[:].bitcast(I32), in_=basis_words.rearrange("g p n -> p g n").bitcast(I32)
-        )
-        base_rows = keep.tile([P, BINS], BF16)
-        nc.sync.dma_start(out=base_rows[:], in_=base_power.partition_broadcast(P))
-        for c in range(1, CLIPS):
-            load_frames(c, 0)
-            load_frames(c, 1)
 
-        def copy_out(engine, out, bank):
-            src = bank[:].rearrange("p (j u m) -> p j m u", j=2, u=2)
-            dst = out.rearrange("p (j m u) -> p j m u", j=2, u=2)
-            if engine == "scalar":
-                nc.scalar.copy(out=dst, in_=src)
+        def load_scales():
+            for q in range(4):
+                nc.sync.dma_start(
+                    out=c_scales[32 * q : 32 * q + 4, :, :].bitcast(I32),
+                    in_=basis_scales[:, 4 * q : 4 * q + 4, :].rearrange("g r n -> r g n").bitcast(I32),
+                )
+
+        def load_rows():
+            nc.sync.dma_start(
+                out=rows_bf[0:GAIN_ROWS, :], in_=frame_gain.rearrange("c (j p) -> (c j) p", p=P)
+            )
+            nc.sync.dma_start(
+                out=rows_bf[GAIN_ROWS : GAIN_ROWS + EQ_ROWS, :],
+                in_=eq.rearrange("(b p) -> b p", p=P),
+            )
+
+        for item in ORDER.split():
+            if item[0] == "x":
+                load_frames(int(item[1]), int(item[2]))
+            elif item[0] == "w":
+                load_basis(int(item[1]))
+            elif item == "s":
+                load_scales()
+            elif item == "r":
+                load_rows()
+            elif item == "e":
+                nc.sync.dma_start(out=eq_rows[:], in_=eq[0:BANK].partition_broadcast(P))
             else:
-                nc.vector.tensor_copy(out=dst, in_=src)
+                load_base(0, BINS)
+        for c in range(2, CLIPS):
+            for j in range(4):
+                load_frames(c, j)
+
+        def copy_on(engine, out, in_):
+            if engine == "gpsimd":
+                for j in range(2):
+                    nc.gpsimd.tensor_scalar(
+                        out=out[:, j], in0=in_[:, j], scalar1=1.0, scalar2=0.0, op0=ALU.mult, op1=ALU.add
+                    )
+            elif engine == "scalar":
+                nc.scalar.copy(out=out, in_=in_)
+            else:
+                nc.vector.tensor_copy(out=out, in_=in_)
+
+        def copy_out(engine, out, bank, n):
+            copy_on(
+                engine,
+                out.rearrange("p (a m u) -> p a m u", a=n, u=2),
+                bank.rearrange("p (a u m) -> p a m u", a=n, u=2),
+            )
 
         x_turned, x_codes, x_scales = {}, {}, {}
 
-        def turn_frames(c, g, h, engine):
-            if h == 0:
-                x_turned[(c, g)] = work.tile(
-                    [P, 2 * T], F32, name="x_turned", tag="x_turned", bufs=3, align_bytes=64
-                )
-            bank = next_bank()
-            for j in range(2):
-                for u in range(2):
-                    nc.tensor.transpose(
-                        bank[:, P * (2 * j + u) : P * (2 * j + u + 1)],
-                        x_raw[(c, h)][:, j, 256 * g + u : 256 * (g + 1) : 2],
-                        ident[:],
-                    )
-            copy_out(engine, x_turned[(c, g)][:, BANK * h : BANK * (h + 1)], bank)
+        held = {}
 
-        def quantize_frames(c, g):
-            codes = work.tile([P, T], U32, name="x_codes", tag="x_codes", bufs=4, align_bytes=64)
-            scales = work.tile([P, T], U8, name="x_scales", tag="x_scales", bufs=4, align_bytes=64)
-            nc.vector.quantize_mx(
-                out=codes[:].bitcast(FP8X4), scales=scales[:], in_=x_turned[(c, g)][:].bitcast(BF16)
+        x_sorted = {}
+
+        def sort_frames(c, j):
+            if 4 * c + j < SORT0 or 4 * c + j >= UNSORT:
+                return
+            words = work.tile([P, K // 2], F32, name="x_sorted", tag="x_sorted", bufs=6)
+            nc.vector.tensor_copy(
+                out=words[:].rearrange("p (g u q) -> p g u q", g=K_PASSES, u=2),
+                in_=x_raw[(c, j)][:].rearrange("p (g q u) -> p g u q", g=K_PASSES, u=2),
             )
-            x_codes[(c, g)], x_scales[(c, g)] = codes, scales
+            x_sorted[(c, j)] = words
+
+        def turn_frames(c, j):
+            bank = next_bank()
+            for g in range(K_PASSES):
+                for u in range(2):
+                    i = 2 * g + u
+                    if 4 * c + j < SORT0 or 4 * c + j >= UNSORT:
+                        src = x_raw[(c, j)][:, 256 * g + u : 256 * (g + 1) : 2]
+                    else:
+                        src = x_sorted[(c, j)][:, P * i : P * (i + 1)]
+                    nc.tensor.transpose(bank[:, P * i : P * (i + 1)], src, ident[:])
+            held[("x", c, j)] = bank
+
+        def copy_frames(c, j, engine="scalar"):
+            turned = work.tile([P, BANK], F32, name="x_turned", tag="x_turned", bufs=6, align_bytes=64)
+            copy_out(engine, turned[:], held[("x", c, j)][:], 2)
+            x_turned[(c, j)] = turned
+
+        def quantize_frames(c, j):
+            for g in range(K_PASSES):
+                if j == 0:
+                    x_codes[(c, g)] = work.tile(
+                        [P, T], U32, name="x_codes", tag="x_codes", bufs=4, align_bytes=64
+                    )
+                    x_scales[(c, g)] = work.tile(
+                        [P, T], U8, name="x_scales", tag="x_scales", bufs=4, align_bytes=64
+                    )
+                nc.vector.quantize_mx(
+                    out=x_codes[(c, g)][:, P * j : P * (j + 1)].bitcast(FP8X4),
+                    scales=x_scales[(c, g)][:, P * j : P * (j + 1)],
+                    in_=x_turned[(c, j)][:, 2 * P * g : 2 * P * (g + 1)].bitcast(BF16),
+                )
 
         used = GAIN_ROWS + EQ_ROWS
-        turn_frames(0, 0, 0, "scalar")
-        turn_frames(0, 0, 1, "vector")
-        turn_frames(0, 1, 0, "scalar")
-        quantize_frames(0, 0)
-        nc.vector.tensor_copy(out=rows_f32[0:used, :], in_=rows_bf[0:used, :])
-        turn_frames(0, 1, 1, "scalar")
         cols = keep.tile([P, used], F32)
-        bank = next_bank()
-        nc.tensor.transpose(bank[:, 0:P], rows_f32[:], ident[:])
-        nc.vector.tensor_copy(out=cols[:], in_=bank[:, 0:used])
-        quantize_frames(0, 1)
 
-        squares, y_rows, y_pairs, y_turned, planes = {}, {}, {}, {}, {}
-
-        def multiply(s):
-            c, grp = divmod(s, GROUPS)
-            for b in range(4):
-                blk = 4 * grp + b
-                bank = next_bank()
-                for g in range(K_PASSES):
-                    nc.tensor.matmul_mx(
-                        out=bank[:],
-                        lhsT=c_words[:, g, 2 * P * blk : 2 * P * (blk + 1)].bitcast(FP4X4),
-                        lhsT_scale=c_scales[:, g, P * blk : P * (blk + 1)],
-                        rhs=x_codes[(c, g)][:].bitcast(FP8X4),
-                        rhs_scale=x_scales[(c, g)][:],
-                        start=(g == 0),
-                        stop=(g == K_PASSES - 1),
-                    )
-                sq = work.tile([P, T], F32, name="squares", tag="squares", bufs=8)
-                nc.scalar.activation(
-                    out=sq[:],
-                    in_=bank[:],
-                    func=ACT.Square,
-                    scale=cols[:, GAIN_ROWS + blk : GAIN_ROWS + blk + 1],
-                )
-                squares[(s, b)] = sq
-
-        def power(s):
-            c, grp = divmod(s, GROUPS)
-            for h in range(2):
-                y = work.tile([P, 2, BANK], F32, name="y_rows", tag="y_rows", bufs=6)
-                for j in range(2):
-                    tile_no = 2 * h + j
-                    bank = next_bank()
-                    for b in range(4):
-                        nc.tensor.transpose(
-                            bank[:, P * b : P * (b + 1)],
-                            squares[(s, b)][:, P * tile_no : P * (tile_no + 1)],
-                            ident[:],
-                        )
-                    nc.vector.scalar_tensor_tensor(
-                        out=y[:, j, :],
-                        in0=bank[:],
-                        scalar=cols[:, 4 * c + tile_no : 4 * c + tile_no + 1],
-                        in1=base_rows[:, BANK * grp : BANK * (grp + 1)],
-                        op0=ALU.mult,
-                        op1=ALU.add,
-                    )
-                dst = out_0[c, 2 * P * h : 2 * P * (h + 1), BANK * grp : BANK * (grp + 1)]
-                nc.sync.dma_start(out=dst.rearrange("(j p) n -> p j n", p=P), in_=y[:])
-                y_rows[(s, h)] = y
-
-        def round_pairs(s, h):
-            pairs = work.tile([P, 2 * BANK], BF16, name="y_pairs", tag="y_pairs", bufs=6)
-            nc.vector.tensor_copy(
-                out=pairs[:].rearrange("p (j u q e) -> p j u q e", j=2, u=2, e=2),
-                in_=y_rows[(s, h)][:].rearrange("p j (q u e) -> p j u q e", u=2, e=2),
-            )
-            y_pairs[(s, h)] = pairs
-
-        def turn_pairs(s, h, engine):
-            if h == 0:
-                y_turned[s] = work.tile(
-                    [P, 2 * T], F32, name="y_turned", tag="y_turned", bufs=3, align_bytes=64
-                )
+        def turn_constants():
             bank = next_bank()
-            words = y_pairs[(s, h)][:].bitcast(F32)
-            for i in range(4):
-                nc.tensor.transpose(
-                    bank[:, P * i : P * (i + 1)], words[:, P * i : P * (i + 1)], ident[:]
-                )
-            copy_out(engine, y_turned[s][:, BANK * h : BANK * (h + 1)], bank)
+            nc.tensor.transpose(bank[:, 0:P], rows_f32[:], ident[:])
+            nc.scalar.copy(out=cols[:], in_=bank[:, 0:used])
 
-        def quantize_power(s):
+        squares, y_rows, y_pairs, y_turned, y_codes, planes = {}, {}, {}, {}, {}, {}
+
+        def multiply_by_frames(c, j):
+            bank = next_bank()
+            for g in range(K_PASSES):
+                nc.tensor.matmul_mx(
+                    out=bank[:],
+                    lhsT=x_codes[(c, g)][:, P * j : P * (j + 1)].bitcast(FP8X4),
+                    lhsT_scale=x_scales[(c, g)][:, P * j : P * (j + 1)],
+                    rhs=c_words[0][:, g, :].bitcast(FP4X4),
+                    rhs_scale=c_scales[:, g, 0:BANK],
+                    start=(g == 0),
+                    stop=(g == K_PASSES - 1),
+                )
+            held[("amp", c, j)] = bank
+
+        amps = {}
+
+        def equalise(c, j):
+            amp = work.tile([P, BANK], F32, name="amp", tag="amp", bufs=4)
+            nc.vector.tensor_tensor(
+                out=amp[:], in0=held[("amp", c, j)][:], in1=eq_rows[:], op=ALU.mult
+            )
+            amps[(c, j)] = amp
+
+        def square_by_frames(c, j):
+            sq = work.tile([P, BANK], F32, name="sq_frames", tag="sq_frames", bufs=4)
+            nc.scalar.activation(out=sq[:], in_=amps[(c, j)][:], func=ACT.Square)
+            squares[(GROUPS * c, j)] = sq
+
+        def multiply_by_bins(s, b):
             c, grp = divmod(s, GROUPS)
-            if grp == 0:
+            blk = 4 * grp + b
+            bank = next_bank()
+            for g in range(K_PASSES):
+                nc.tensor.matmul_mx(
+                    out=bank[:],
+                    lhsT=c_words[grp][:, g, 2 * P * b : 2 * P * (b + 1)].bitcast(FP4X4),
+                    lhsT_scale=c_scales[:, g, P * blk : P * (blk + 1)],
+                    rhs=x_codes[(c, g)][:].bitcast(FP8X4),
+                    rhs_scale=x_scales[(c, g)][:],
+                    start=(g == 0),
+                    stop=(g == K_PASSES - 1),
+                )
+            held[("bins", s, b)] = bank
+
+        def square_by_bins(s, b):
+            sq = work.tile([P, T], F32, name="sq_bins", tag="sq_bins", bufs=8)
+            col = GAIN_ROWS + 4 * (s % GROUPS) + b
+            nc.scalar.activation(
+                out=sq[:], in_=held[("bins", s, b)][:], func=ACT.Square, scale=cols[:, col : col + 1]
+            )
+            squares[(s, b)] = sq
+
+        def turn_squares(s, j, blocks):
+            if blocks[0] == 0:
+                held[("sq", s, j)] = next_bank()
+            bank = held[("sq", s, j)]
+            for b in blocks:
+                nc.tensor.transpose(
+                    bank[:, P * b : P * (b + 1)], squares[(s, b)][:, P * j : P * (j + 1)], ident[:]
+                )
+
+        def power(s, j):
+            c, grp = divmod(s, GROUPS)
+            h, i = divmod(j, 2)
+            if i == 0:
+                y_rows[(s, h)] = work.tile([P, 2 * BANK], F32, name="y_rows", tag="y_rows", bufs=6)
+            y = y_rows[(s, h)]
+            src = squares[(s, j)] if s in TOK else held[("sq", s, j)]
+            nc.vector.scalar_tensor_tensor(
+                out=y[:, BANK * i : BANK * (i + 1)],
+                in0=src[:],
+                scalar=cols[:, 4 * c + j : 4 * c + j + 1],
+                in1=base_rows[grp],
+                op0=ALU.mult,
+                op1=ALU.add,
+            )
+            if i == 1:
+                dst = out_0[c, 2 * P * h : 2 * P * (h + 1), BANK * grp : BANK * (grp + 1)]
+                nc.sync.dma_start(
+                    out=dst.rearrange("(j p) n -> p j n", p=P),
+                    in_=y[:].rearrange("p (j n) -> p j n", j=2),
+                )
+
+        def round_pairs(s, j, n, engine):
+            pairs = work.tile([P, n * BANK], BF16, name="y_pairs", tag="y_pairs", bufs=8)
+            src = y_rows[(s, j // 2)][:, BANK * (j % 2) : BANK * (j % 2 + n)]
+            copy_on(
+                engine,
+                pairs[:].rearrange("p (j u q e) -> p j u q e", j=n, u=2, e=2),
+                src.rearrange("p (j q u e) -> p j u q e", j=n, u=2, e=2),
+            )
+            for i in range(n):
+                y_pairs[(s, j + i)] = pairs[:, BANK * i : BANK * (i + 1)].bitcast(F32)
+
+        def turn_pairs(s, j, n):
+            bank = next_bank()
+            for i in range(n):
+                for u in range(2):
+                    nc.tensor.transpose(
+                        bank[:, P * (2 * i + u) : P * (2 * i + u + 1)],
+                        y_pairs[(s, j + i)][:, P * u : P * (u + 1)],
+                        ident[:],
+                    )
+            held[("y", s, j)] = bank
+
+        def copy_pairs(s, j, n, engine="scalar"):
+            turned = work.tile(
+                [P, 2 * P * n], F32, name="y_turned", tag="y_turned", bufs=8, align_bytes=64
+            )
+            copy_out(engine, turned[:], held[("y", s, j)][:, 0 : 2 * P * n], n)
+            y_turned[(s, j)] = turned
+
+        def store_codes(s, first, last):
+            c, grp = divmod(s, GROUPS)
+            dst = out_1[grp, :, T * c + first : T * c + last, :].rearrange("p m t -> p (m t)")
+            nc.sync.dma_start(out=dst.bitcast(I32), in_=y_codes[s][:, first:last].bitcast(I32))
+
+        done = {}
+
+        def quantize_power(s, j, n):
+            c, grp = divmod(s, GROUPS)
+            if c not in planes:
                 planes[c] = work.tile(
                     [P, GROUPS, T], U8, name="y_scales", tag="y_scales", bufs=2, align_bytes=64
                 )
-            codes = work.tile([P, T], U32, name="y_codes", tag="y_codes", bufs=3, align_bytes=64)
+            if j == 0:
+                y_codes[s] = work.tile(
+                    [P, T], U32, name="y_codes", tag="y_codes", bufs=4, align_bytes=64
+                )
             nc.vector.quantize_mx(
-                out=codes[:].bitcast(FP8X4),
-                scales=planes[c][:, grp, :],
-                in_=y_turned[s][:].bitcast(BF16),
+                out=y_codes[s][:, P * j : P * (j + n)].bitcast(FP8X4),
+                scales=planes[c][:, grp, P * j : P * (j + n)],
+                in_=y_turned[(s, j)][:].bitcast(BF16),
             )
-            dst = out_1[grp, :, T * c : T * (c + 1), :].rearrange("p m t -> p (m t)")
-            nc.sync.dma_start(out=dst.bitcast(I32), in_=codes[:].bitcast(I32))
-            if grp == GROUPS - 1:
+            if s == UNITS - 1 and j + n >= 3:
+                store_codes(s, 0 if j + n == 3 else 3 * P, P * (j + n))
+            elif j + n == 4:
+                store_codes(s, 0, T)
+            done[c] = done.get(c, 0) + n
+            if done[c] == 4 * GROUPS:
                 for q in range(4):
                     rows = out_2[:, 4 * q : 4 * q + 4, T * c : T * (c + 1)]
                     nc.sync.dma_start(
@@ -224,32 +349,86 @@ def tile_cosine_power_for_mel_g4_kernel(
                         in_=planes[c][32 * q : 32 * q + 4, :, :].bitcast(I32),
                     )
 
-        for s in range(UNITS):
+        turn_frames(0, 0)
+        copy_frames(0, 0, "scalar")
+        for j in range(1, 4):
+            sort_frames(0, j)
+            turn_frames(0, j)
+            copy_frames(0, j, "scalar")
+        for j in range(4):
+            quantize_frames(0, j)
+            multiply_by_frames(0, j)
+        nc.scalar.copy(out=rows_f32[0:used, :], in_=rows_bf[0:used, :])
+        equalise(0, 0)
+        square_by_frames(0, 0)
+        turn_constants()
+        for j in range(1, 4):
+            equalise(0, j)
+            if j < SQ0:
+                square_by_frames(0, j)
+        for j in range(4):
+            sort_frames(1, j)
+
+        last = UNITS - 1
+        for s in range(1, UNITS):
             c, grp = divmod(s, GROUPS)
-            feeds_next = c + 1 < CLIPS and grp < K_PASSES
-            multiply(s)
-            if feeds_next:
-                turn_frames(c + 1, grp, 0, "scalar")
-                turn_frames(c + 1, grp, 1, "scalar")
-            if s >= PLANE_LAG:
-                turn_pairs(s - PLANE_LAG, 0, "scalar")
-                turn_pairs(s - PLANE_LAG, 1, "scalar")
-            if s == UNITS - 1:
-                turn_pairs(s - 1, 0, "scalar")
-                turn_pairs(s - 1, 1, "scalar")
-            power(s)
-            if s == UNITS - 1:
-                round_pairs(s, 0)
-                round_pairs(s, 1)
-                turn_pairs(s, 0, "scalar")
-                turn_pairs(s, 1, "scalar")
-                quantize_power(s - 2)
-                quantize_power(s - 1)
-                quantize_power(s)
+            if c == 0:
+                tiles = range(4) if s == 1 else ()
             else:
-                if s >= PLANE_LAG:
-                    quantize_power(s - PLANE_LAG)
-                round_pairs(s, 0)
-                round_pairs(s, 1)
-                if feeds_next:
-                    quantize_frames(c + 1, grp)
+                tiles = (2 * grp, 2 * grp + 1) if c + 1 < CLIPS and grp < 2 else ()
+            for b in range(4):
+                multiply_by_bins(s, b)
+                square_by_bins(s, b)
+            if s == 1:
+                for j in range(SQ0, 4):
+                    square_by_frames(0, j)
+                power(0, 0)
+                power(0, 1)
+            else:
+                round_pairs(s - 1, 0, 2, "vector")
+                round_pairs(s - 1, 2, 2, "scalar" if s in SC else "vector")
+            if s >= 3:
+                quantize_power(s - 3, 0, 2)
+                quantize_power(s - 3, 2, 2)
+            nc_, ng = divmod(s + 1, GROUPS)
+            for j in tiles:
+                turn_frames(c + 1, j)
+                copy_frames(c + 1, j)
+            if nc_ + 1 < CLIPS and ng < 2 and s > 1:
+                sort_frames(nc_ + 1, 2 * ng)
+                sort_frames(nc_ + 1, 2 * ng + 1)
+            if s >= 2:
+                for j in (0, 2):
+                    turn_pairs(s - 2, j, 2)
+                    copy_pairs(s - 2, j, 2)
+            if s == last:
+                for j in (0, 2):
+                    turn_pairs(s - 1, j, 2)
+                    copy_pairs(s - 1, j, 2)
+            turn_squares(s, 0, (0, 1, 2))
+            turn_squares(s, 1, (0, 1, 2))
+            for j in range(4):
+                turn_squares(s, j, (3,) if j < 2 else (0, 1, 2, 3))
+                power(s, j)
+                if s == last:
+                    round_pairs(s, j, 1, "scalar" if j < 3 else "vector")
+            if s == 1:
+                power(0, 2)
+                power(0, 3)
+                round_pairs(0, 0, 2, R0[0])
+                round_pairs(0, 2, 2, R0[1])
+            for j in tiles:
+                quantize_frames(c + 1, j)
+        turn_pairs(s, 0, 2)
+        turn_pairs(s, 2, 1)
+        turn_pairs(s, 3, 1)
+        copy_pairs(s, 0, 2)
+        for j in (0, 2):
+            quantize_power(s - 2, j, 2)
+        copy_pairs(s, 2, 1, T11)
+        copy_pairs(s, 3, 1)
+        for j in (0, 2):
+            quantize_power(s - 1, j, 2)
+        quantize_power(s, 0, 2)
+        quantize_power(s, 2, 1)
+        quantize_power(s, 3, 1)

@@ -25,12 +25,16 @@ UNITS = CLIPS * GROUPS
 GAIN_ROWS = CLIPS * T // P
 EQ_ROWS = BINS // P
 CAST = (("scalar", "scalar"), ("vector", "vector"), ("vector", "vector"))
-TOK = (0,)
+TOK = ()
+NP = 3
+QS = 2
 SORT0 = 1
 SCAST = (2,)
 R0 = ("vector", "vector")
-ORDER = "x00 x01 x02 x03 w0 s e r w1 x10 x11 x12 x13 b w2"
-UNSORT = 16
+ORDER = "x00 x01 x02 x03 w0 s r x10 x12 b w1 w2"
+SORT = True
+GT = 2
+TAILG = 0
 SQ0 = 2
 SC = (2, 5, 8, 9, 10)
 T9 = "scalar"
@@ -58,9 +62,13 @@ def tile_cosine_power_for_mel_g4_kernel(
         frame_words = frames.bitcast(F32)
         x_raw = {}
 
-        def load_frames(c, j):
-            raw = work.tile([P, K // 2], F32, name="x_raw", tag="x_raw", bufs=4 * CLIPS)
-            nc.sync.dma_start(out=raw[:], in_=frame_words[c, P * j : P * (j + 1), :])
+        def load_frames(c, j, n=1):
+            raw = work.tile([P, n * K // 2], F32, name="x_raw", tag="x_raw", bufs=10)
+            rows = frame_words[c, P * j : P * (j + n), :]
+            nc.sync.dma_start(
+                out=raw[:].rearrange("p (j w) -> p j w", j=n),
+                in_=rows.rearrange("(j p) w -> p j w", p=P),
+            )
             x_raw[(c, j)] = raw
 
         c_words = {}
@@ -111,7 +119,7 @@ def tile_cosine_power_for_mel_g4_kernel(
 
         for item in ORDER.split():
             if item[0] == "x":
-                load_frames(int(item[1]), int(item[2]))
+                load_frames(int(item[1]), int(item[2]), 1 if item[1] == "0" else 2)
             elif item[0] == "w":
                 load_basis(int(item[1]))
             elif item == "s":
@@ -123,15 +131,14 @@ def tile_cosine_power_for_mel_g4_kernel(
             else:
                 load_base(0, BINS)
         for c in range(2, CLIPS):
-            for j in range(4):
-                load_frames(c, j)
+            for j in (0, 2):
+                load_frames(c, j, 2)
 
         def copy_on(engine, out, in_):
             if engine == "gpsimd":
-                for j in range(2):
-                    nc.gpsimd.tensor_scalar(
-                        out=out[:, j], in0=in_[:, j], scalar1=1.0, scalar2=0.0, op0=ALU.mult, op1=ALU.add
-                    )
+                nc.gpsimd.tensor_scalar(
+                    out=out[:, 0], in0=in_[:, 0], scalar1=1.0, scalar2=0.0, op0=ALU.mult, op1=ALU.add
+                )
             elif engine == "scalar":
                 nc.scalar.copy(out=out, in_=in_)
             else:
@@ -150,47 +157,71 @@ def tile_cosine_power_for_mel_g4_kernel(
 
         x_sorted = {}
 
-        def sort_frames(c, j):
-            if 4 * c + j < SORT0 or 4 * c + j >= UNSORT:
+        def sort_frames(c, j, n):
+            if not (SORT if c > 0 else True):
+                x_sorted[(c, j)] = None
                 return
-            words = work.tile([P, K // 2], F32, name="x_sorted", tag="x_sorted", bufs=6)
+            words = work.tile([P, n * K // 2], F32, name="x_sorted", tag="x_sorted", bufs=4)
             nc.vector.tensor_copy(
-                out=words[:].rearrange("p (g u q) -> p g u q", g=K_PASSES, u=2),
-                in_=x_raw[(c, j)][:].rearrange("p (g q u) -> p g u q", g=K_PASSES, u=2),
+                out=words[:].rearrange("p (g u q) -> p g u q", q=P, u=2),
+                in_=x_raw[(c, j)][:].rearrange("p (g q u) -> p g u q", q=P, u=2),
             )
             x_sorted[(c, j)] = words
 
-        def turn_frames(c, j):
+        def frame_slice(c, first, a, u):
+            if x_sorted[(c, first)] is None:
+                return x_raw[(c, first)][:, 256 * a + u : 256 * (a + 1) : 2]
+            return x_sorted[(c, first)][:, P * (2 * a + u) : P * (2 * a + u + 1)]
+
+        def turn_frames(key, c, first, parts):
             bank = next_bank()
-            for g in range(K_PASSES):
+            for i, a in enumerate(parts):
                 for u in range(2):
-                    i = 2 * g + u
-                    if 4 * c + j < SORT0 or 4 * c + j >= UNSORT:
-                        src = x_raw[(c, j)][:, 256 * g + u : 256 * (g + 1) : 2]
-                    else:
-                        src = x_sorted[(c, j)][:, P * i : P * (i + 1)]
-                    nc.tensor.transpose(bank[:, P * i : P * (i + 1)], src, ident[:])
-            held[("x", c, j)] = bank
+                    nc.tensor.transpose(
+                        bank[:, P * (2 * i + u) : P * (2 * i + u + 1)],
+                        frame_slice(c, first, a, u),
+                        ident[:],
+                    )
+            held[key] = bank
 
-        def copy_frames(c, j, engine="scalar"):
-            turned = work.tile([P, BANK], F32, name="x_turned", tag="x_turned", bufs=6, align_bytes=64)
-            copy_out(engine, turned[:], held[("x", c, j)][:], 2)
-            x_turned[(c, j)] = turned
-
-        def quantize_frames(c, j):
+        def codes_of(c):
             for g in range(K_PASSES):
-                if j == 0:
-                    x_codes[(c, g)] = work.tile(
-                        [P, T], U32, name="x_codes", tag="x_codes", bufs=4, align_bytes=64
-                    )
-                    x_scales[(c, g)] = work.tile(
-                        [P, T], U8, name="x_scales", tag="x_scales", bufs=4, align_bytes=64
-                    )
-                nc.vector.quantize_mx(
-                    out=x_codes[(c, g)][:, P * j : P * (j + 1)].bitcast(FP8X4),
-                    scales=x_scales[(c, g)][:, P * j : P * (j + 1)],
-                    in_=x_turned[(c, j)][:, 2 * P * g : 2 * P * (g + 1)].bitcast(BF16),
+                x_codes[(c, g)] = work.tile(
+                    [P, T], U32, name="x_codes", tag="x_codes", bufs=4, align_bytes=64
                 )
+                x_scales[(c, g)] = work.tile(
+                    [P, T], U8, name="x_scales", tag="x_scales", bufs=4, align_bytes=64
+                )
+
+        def turn_tile(j):
+            turn_frames(("x", j), 0, j, (0, 1))
+            turned = work.tile([P, BANK], F32, name="x_turned0", tag="x_turned0", bufs=4, align_bytes=64)
+            copy_out("scalar", turned[:], held[("x", j)][:], 2)
+            x_turned[j] = turned
+
+        def quantize_tile(j):
+            for g in range(K_PASSES):
+                nc.vector.quantize_mx(
+                    out=x_codes[(0, g)][:, P * j : P * (j + 1)].bitcast(FP8X4),
+                    scales=x_scales[(0, g)][:, P * j : P * (j + 1)],
+                    in_=x_turned[j][:, 2 * P * g : 2 * P * (g + 1)].bitcast(BF16),
+                )
+
+        def turn_pass(c, g):
+            turned = work.tile([P, 2 * T], F32, name="x_turned", tag="x_turned", bufs=3, align_bytes=64)
+            for h in range(2):
+                turn_frames(("x", c, g, h), c, 2 * h, (g, 2 + g))
+                copy_out("scalar", turned[:, BANK * h : BANK * (h + 1)], held[("x", c, g, h)][:], 2)
+            x_turned[(c, g)] = turned
+
+        def quantize_pass(c, g):
+            if g == 0:
+                codes_of(c)
+            nc.vector.quantize_mx(
+                out=x_codes[(c, g)][:].bitcast(FP8X4),
+                scales=x_scales[(c, g)][:],
+                in_=x_turned[(c, g)][:].bitcast(BF16),
+            )
 
         used = GAIN_ROWS + EQ_ROWS
         cols = keep.tile([P, used], F32)
@@ -265,29 +296,28 @@ def tile_cosine_power_for_mel_g4_kernel(
 
         def power(s, j):
             c, grp = divmod(s, GROUPS)
-            h, i = divmod(j, 2)
-            if i == 0:
-                y_rows[(s, h)] = work.tile([P, 2 * BANK], F32, name="y_rows", tag="y_rows", bufs=6)
-            y = y_rows[(s, h)]
+            if j == 0:
+                y_rows[s] = work.tile([P, 4 * BANK], F32, name="y_rows", tag="y_rows", bufs=4)
+            y = y_rows[s]
             src = squares[(s, j)] if s in TOK else held[("sq", s, j)]
             nc.vector.scalar_tensor_tensor(
-                out=y[:, BANK * i : BANK * (i + 1)],
+                out=y[:, BANK * j : BANK * (j + 1)],
                 in0=src[:],
                 scalar=cols[:, 4 * c + j : 4 * c + j + 1],
                 in1=base_rows[grp],
                 op0=ALU.mult,
                 op1=ALU.add,
             )
-            if i == 1:
-                dst = out_0[c, 2 * P * h : 2 * P * (h + 1), BANK * grp : BANK * (grp + 1)]
+            if j % 2 == 1:
+                dst = out_0[c, P * (j - 1) : P * (j + 1), BANK * grp : BANK * (grp + 1)]
                 nc.sync.dma_start(
                     out=dst.rearrange("(j p) n -> p j n", p=P),
-                    in_=y[:].rearrange("p (j n) -> p j n", j=2),
+                    in_=y[:, BANK * (j - 1) : BANK * (j + 1)].rearrange("p (j n) -> p j n", j=2),
                 )
 
         def round_pairs(s, j, n, engine):
-            pairs = work.tile([P, n * BANK], BF16, name="y_pairs", tag="y_pairs", bufs=8)
-            src = y_rows[(s, j // 2)][:, BANK * (j % 2) : BANK * (j % 2 + n)]
+            pairs = work.tile([P, n * BANK], BF16, name="y_pairs", tag="y_pairs", bufs=9)
+            src = y_rows[s][:, BANK * j : BANK * (j + n)]
             copy_on(
                 engine,
                 pairs[:].rearrange("p (j u q e) -> p j u q e", j=n, u=2, e=2),
@@ -308,11 +338,16 @@ def tile_cosine_power_for_mel_g4_kernel(
             held[("y", s, j)] = bank
 
         def copy_pairs(s, j, n, engine="scalar"):
-            turned = work.tile(
-                [P, 2 * P * n], F32, name="y_turned", tag="y_turned", bufs=8, align_bytes=64
+            if j == 0:
+                y_turned[s] = work.tile(
+                    [P, 2 * T], F32, name="y_turned", tag="y_turned", bufs=4, align_bytes=64
+                )
+            copy_out(
+                engine,
+                y_turned[s][:, 2 * P * j : 2 * P * (j + n)],
+                held[("y", s, j)][:, 0 : 2 * P * n],
+                n,
             )
-            copy_out(engine, turned[:], held[("y", s, j)][:, 0 : 2 * P * n], n)
-            y_turned[(s, j)] = turned
 
         def store_codes(s, first, last):
             c, grp = divmod(s, GROUPS)
@@ -334,7 +369,7 @@ def tile_cosine_power_for_mel_g4_kernel(
             nc.vector.quantize_mx(
                 out=y_codes[s][:, P * j : P * (j + n)].bitcast(FP8X4),
                 scales=planes[c][:, grp, P * j : P * (j + n)],
-                in_=y_turned[(s, j)][:].bitcast(BF16),
+                in_=y_turned[s][:, 2 * P * j : 2 * P * (j + n)].bitcast(BF16),
             )
             if s == UNITS - 1 and j + n >= 3:
                 store_codes(s, 0 if j + n == 3 else 3 * P, P * (j + n))
@@ -344,91 +379,94 @@ def tile_cosine_power_for_mel_g4_kernel(
             if done[c] == 4 * GROUPS:
                 for q in range(4):
                     rows = out_2[:, 4 * q : 4 * q + 4, T * c : T * (c + 1)]
-                    nc.sync.dma_start(
+                    queue = nc.scalar if c == CLIPS - 1 and q < QS else nc.sync
+                    queue.dma_start(
                         out=rows.rearrange("g r m -> r g m").bitcast(I32),
                         in_=planes[c][32 * q : 32 * q + 4, :, :].bitcast(I32),
                     )
 
-        turn_frames(0, 0)
-        copy_frames(0, 0, "scalar")
-        for j in range(1, 4):
-            sort_frames(0, j)
-            turn_frames(0, j)
-            copy_frames(0, j, "scalar")
+        codes_of(0)
         for j in range(4):
-            quantize_frames(0, j)
-            multiply_by_frames(0, j)
+            sort_frames(0, j, 1)
+            turn_tile(j)
+        for j in range(4):
+            quantize_tile(j)
+            if TOK:
+                multiply_by_frames(0, j)
         nc.scalar.copy(out=rows_f32[0:used, :], in_=rows_bf[0:used, :])
-        equalise(0, 0)
-        square_by_frames(0, 0)
+        if TOK:
+            equalise(0, 0)
+            square_by_frames(0, 0)
         turn_constants()
-        for j in range(1, 4):
-            equalise(0, j)
-            if j < SQ0:
-                square_by_frames(0, j)
-        for j in range(4):
-            sort_frames(1, j)
+        if TOK:
+            for j in range(1, 4):
+                equalise(0, j)
+                if j < SQ0:
+                    square_by_frames(0, j)
+        sort_frames(1, 0, 2)
+        sort_frames(1, 2, 2)
 
         last = UNITS - 1
-        for s in range(1, UNITS):
+        first = len(TOK)
+        for s in range(first, UNITS):
             c, grp = divmod(s, GROUPS)
-            if c == 0:
-                tiles = range(4) if s == 1 else ()
+            if c == 0 and TOK:
+                passes = (0, 1) if s == 1 else ()
             else:
-                tiles = (2 * grp, 2 * grp + 1) if c + 1 < CLIPS and grp < 2 else ()
+                passes = (grp,) if c + 1 < CLIPS and grp < 2 else ()
             for b in range(4):
                 multiply_by_bins(s, b)
                 square_by_bins(s, b)
-            if s == 1:
+            if s == 1 and TOK:
                 for j in range(SQ0, 4):
                     square_by_frames(0, j)
                 power(0, 0)
                 power(0, 1)
-            else:
-                round_pairs(s - 1, 0, 2, "vector")
-                round_pairs(s - 1, 2, 2, "scalar" if s in SC else "vector")
+            elif s >= 1:
+                if s in SC and GT == 0:
+                    round_pairs(s - 1, 0, 2, "vector")
+                    round_pairs(s - 1, 2, 2, "scalar")
+                else:
+                    round_pairs(s - 1, GT, 4 - GT, "vector")
             if s >= 3:
-                quantize_power(s - 3, 0, 2)
-                quantize_power(s - 3, 2, 2)
-            nc_, ng = divmod(s + 1, GROUPS)
-            for j in tiles:
-                turn_frames(c + 1, j)
-                copy_frames(c + 1, j)
-            if nc_ + 1 < CLIPS and ng < 2 and s > 1:
-                sort_frames(nc_ + 1, 2 * ng)
-                sort_frames(nc_ + 1, 2 * ng + 1)
+                quantize_power(s - 3, 0, 4)
+            for g in passes:
+                turn_pass(c + 1, g)
+            if grp == 2 and c + 2 < CLIPS:
+                sort_frames(c + 2, 0, 2)
+                sort_frames(c + 2, 2, 2)
             if s >= 2:
                 for j in (0, 2):
-                    turn_pairs(s - 2, j, 2)
-                    copy_pairs(s - 2, j, 2)
+                    turn_pairs(s - 1 if s == last else s - 2, j, 2)
+                    copy_pairs(s - 1 if s == last else s - 2, j, 2)
             if s == last:
+                quantize_power(s - 2, 0, 4)
+            for j in range(NP):
+                turn_squares(s, j, (0, 1, 2))
+            for j in range(4):
+                turn_squares(s, j, (3,) if j < NP else (0, 1, 2, 3))
+                power(s, j)
+                if s == last:
+                    round_pairs(s, j, 1, "gpsimd" if j < TAILG else "scalar" if j < 3 else "vector")
+                elif j < GT:
+                    round_pairs(s, j, 1, "gpsimd")
+            if s == 1 and TOK:
+                power(0, 2)
+                power(0, 3)
+                round_pairs(0, 0, 4, "vector")
+            if s == last - 1:
                 for j in (0, 2):
                     turn_pairs(s - 1, j, 2)
                     copy_pairs(s - 1, j, 2)
-            turn_squares(s, 0, (0, 1, 2))
-            turn_squares(s, 1, (0, 1, 2))
-            for j in range(4):
-                turn_squares(s, j, (3,) if j < 2 else (0, 1, 2, 3))
-                power(s, j)
-                if s == last:
-                    round_pairs(s, j, 1, "scalar" if j < 3 else "vector")
-            if s == 1:
-                power(0, 2)
-                power(0, 3)
-                round_pairs(0, 0, 2, R0[0])
-                round_pairs(0, 2, 2, R0[1])
-            for j in tiles:
-                quantize_frames(c + 1, j)
+            for g in passes:
+                quantize_pass(c + 1, g)
         turn_pairs(s, 0, 2)
         turn_pairs(s, 2, 1)
         turn_pairs(s, 3, 1)
         copy_pairs(s, 0, 2)
-        for j in (0, 2):
-            quantize_power(s - 2, j, 2)
         copy_pairs(s, 2, 1, T11)
         copy_pairs(s, 3, 1)
-        for j in (0, 2):
-            quantize_power(s - 1, j, 2)
+        quantize_power(s - 1, 0, 4)
         quantize_power(s, 0, 2)
         quantize_power(s, 2, 1)
         quantize_power(s, 3, 1)

@@ -19,27 +19,19 @@ ACT = mybir.ActivationFunctionType
 P = 128
 BANK = 512
 BANKS = 8
-K_PASSES = K // 512
-GROUPS = BINS // 512
+PASSES = K // 512
+PAIRS = 256
+TILES = T // P
+BLOCKS = BANK // P
+GROUPS = BINS // BANK
 UNITS = CLIPS * GROUPS
-GAIN_ROWS = CLIPS * T // P
+QUADRANTS = 4
+X_LOADS = TILES + (CLIPS - 1) * TILES // 2
+GAIN_ROWS = CLIPS * TILES
 EQ_ROWS = BINS // P
-CAST = (("scalar", "scalar"), ("vector", "vector"), ("vector", "vector"))
-TOK = ()
-NP = 3
-QS = 2
-SORT0 = 1
-SCAST = (2,)
-R0 = ("vector", "vector")
-ORDER = "x00 x01 x02 x03 w0 s r x10 x12 b w1 w2"
-SORT = True
-GT = 2
-TAILG = 0
-SQ0 = 2
-SC = (2, 5, 8, 9, 10)
-T9 = "scalar"
-T11 = "scalar"
-FEED0 = 0
+GPSIMD_TILES = 2
+LAST_UNIT_ROUNDERS = ("scalar", "scalar", "scalar", "vector")
+EARLY_TILES = 3
 
 
 def tile_cosine_power_for_mel_g4_kernel(
@@ -48,425 +40,314 @@ def tile_cosine_power_for_mel_g4_kernel(
     nc = tc.nc
     with ExitStack() as ctx:
         keep = ctx.enter_context(tc.tile_pool(name="keep", bufs=1))
-        work = ctx.enter_context(tc.tile_pool(name="work", bufs=2))
+        work = ctx.enter_context(tc.tile_pool(name="work", bufs=1))
         psum = ctx.enter_context(tc.psum_pool(name="psum", bufs=1))
         ctx.enter_context(tc.manual_schedule())
 
-        bank_count = [0]
+        banks_taken = []
 
         def next_bank():
-            tag = "bank%d" % (bank_count[0] % BANKS)
-            bank_count[0] = bank_count[0] + 1
+            tag = "bank%d" % (len(banks_taken) % BANKS)
+            banks_taken.append(tag)
             return psum.tile([P, BANK], F32, name=tag, tag=tag)
 
-        frame_words = frames.bitcast(F32)
-        x_raw = {}
+        ident = keep.tile([P, P], F32, name="ident")
+        make_identity(nc, ident[:])
+        rows_f32 = keep.tile([P, P], F32, name="rows_f32")
+        c_scales = keep.tile([P, PASSES, BINS], U8, name="c_scales", align_bytes=64)
+        nc.vector.memset(c_scales[:].rearrange("p g n -> p (g n)").bitcast(I32), 0)
+        nc.vector.memset(rows_f32[:], 0.0)
+        rows_bf16 = keep.tile([P, P], BF16, name="rows_bf16")
 
-        def load_frames(c, j, n=1):
-            raw = work.tile([P, n * K // 2], F32, name="x_raw", tag="x_raw", bufs=10)
-            rows = frame_words[c, P * j : P * (j + n), :]
+        frame_pairs = frames.bitcast(F32)
+        x_raw, x_sorted, c_words = {}, {}, {}
+
+        def load_frames(c, first, count):
+            raw = work.tile([P, count * PASSES * PAIRS], F32, name="x_raw", tag="x_raw", bufs=X_LOADS)
+            src = frame_pairs[c, P * first : P * (first + count), :]
             nc.sync.dma_start(
-                out=raw[:].rearrange("p (j w) -> p j w", j=n),
-                in_=rows.rearrange("(j p) w -> p j w", p=P),
+                out=raw[:].rearrange("p (j w) -> p j w", j=count),
+                in_=src.rearrange("(j p) w -> p j w", p=P),
             )
-            x_raw[(c, j)] = raw
-
-        c_words = {}
+            x_raw[(c, first)] = raw
 
         def load_basis(grp):
-            words = keep.tile(
-                [P, K_PASSES, 2 * BANK], U8, name="c_words%d" % grp, align_bytes=64
-            )
+            words = keep.tile([P, PASSES, 2 * BANK], U8, name="c_words%d" % grp, align_bytes=64)
             src = basis_words[:, :, 2 * BANK * grp : 2 * BANK * (grp + 1)]
             nc.sync.dma_start(
                 out=words[:].bitcast(I32), in_=src.rearrange("g p n -> p g n").bitcast(I32)
             )
             c_words[grp] = words
 
-        ident = keep.tile([P, P], F32)
-        make_identity(nc, ident[:])
-        rows_f32 = keep.tile([P, P], F32)
-        c_scales = keep.tile([P, K_PASSES, BINS], U8, align_bytes=64)
-        nc.vector.memset(c_scales[:].rearrange("p g n -> p (g n)").bitcast(I32), 0)
-        nc.vector.memset(rows_f32[:], 0.0)
-
-        base_rows = {}
-
-        def load_base(first, last):
-            rows = keep.tile([P, last - first], BF16, name="base_rows%d" % first)
-            nc.sync.dma_start(out=rows[:], in_=base_power[first:last].partition_broadcast(P))
-            for grp in range(first // BANK, last // BANK):
-                base_rows[grp] = rows[:, BANK * grp - first : BANK * (grp + 1) - first]
-
-        eq_rows = keep.tile([P, BANK], BF16)
-        rows_bf = keep.tile([P, P], BF16)
-
-        def load_scales():
-            for q in range(4):
-                nc.sync.dma_start(
-                    out=c_scales[32 * q : 32 * q + 4, :, :].bitcast(I32),
-                    in_=basis_scales[:, 4 * q : 4 * q + 4, :].rearrange("g r n -> r g n").bitcast(I32),
-                )
-
-        def load_rows():
+        for j in range(TILES):
+            load_frames(0, j, 1)
+        for quad in range(QUADRANTS):
+            src = basis_scales[:, 4 * quad : 4 * quad + 4, :].rearrange("g r n -> r g n")
             nc.sync.dma_start(
-                out=rows_bf[0:GAIN_ROWS, :], in_=frame_gain.rearrange("c (j p) -> (c j) p", p=P)
+                out=c_scales[32 * quad : 32 * quad + 4, :, :].bitcast(I32), in_=src.bitcast(I32)
             )
-            nc.sync.dma_start(
-                out=rows_bf[GAIN_ROWS : GAIN_ROWS + EQ_ROWS, :],
-                in_=eq.rearrange("(b p) -> b p", p=P),
-            )
-
-        for item in ORDER.split():
-            if item[0] == "x":
-                load_frames(int(item[1]), int(item[2]), 1 if item[1] == "0" else 2)
-            elif item[0] == "w":
-                load_basis(int(item[1]))
-            elif item == "s":
-                load_scales()
-            elif item == "r":
-                load_rows()
-            elif item == "e":
-                nc.sync.dma_start(out=eq_rows[:], in_=eq[0:BANK].partition_broadcast(P))
-            else:
-                load_base(0, BINS)
+        load_basis(0)
+        const_rows = GAIN_ROWS + EQ_ROWS
+        nc.sync.dma_start(
+            out=rows_bf16[0:GAIN_ROWS, :], in_=frame_gain.rearrange("c (j p) -> (c j) p", p=P)
+        )
+        nc.sync.dma_start(
+            out=rows_bf16[GAIN_ROWS:const_rows, :], in_=eq.rearrange("(b p) -> b p", p=P)
+        )
+        for j in (0, 2):
+            load_frames(1, j, 2)
+        load_basis(1)
+        base_rows = keep.tile([P, BINS], BF16, name="base_rows")
+        nc.sync.dma_start(out=base_rows[:], in_=base_power.partition_broadcast(P))
+        load_basis(2)
         for c in range(2, CLIPS):
             for j in (0, 2):
                 load_frames(c, j, 2)
 
-        def copy_on(engine, out, in_):
-            if engine == "gpsimd":
-                nc.gpsimd.tensor_scalar(
-                    out=out[:, 0], in0=in_[:, 0], scalar1=1.0, scalar2=0.0, op0=ALU.mult, op1=ALU.add
-                )
-            elif engine == "scalar":
-                nc.scalar.copy(out=out, in_=in_)
-            else:
-                nc.vector.tensor_copy(out=out, in_=in_)
-
-        def copy_out(engine, out, bank, n):
-            copy_on(
-                engine,
-                out.rearrange("p (a m u) -> p a m u", a=n, u=2),
-                bank.rearrange("p (a u m) -> p a m u", a=n, u=2),
-            )
-
         x_turned, x_codes, x_scales = {}, {}, {}
 
-        held = {}
-
-        x_sorted = {}
-
-        def sort_frames(c, j, n):
-            if not (SORT if c > 0 else True):
-                x_sorted[(c, j)] = None
-                return
-            words = work.tile([P, n * K // 2], F32, name="x_sorted", tag="x_sorted", bufs=4)
-            nc.vector.tensor_copy(
-                out=words[:].rearrange("p (g u q) -> p g u q", q=P, u=2),
-                in_=x_raw[(c, j)][:].rearrange("p (g q u) -> p g u q", q=P, u=2),
+        def sort_frames(c, first, count):
+            ordered = work.tile(
+                [P, count * PASSES * PAIRS], F32, name="x_sorted", tag="x_sorted", bufs=4
             )
-            x_sorted[(c, j)] = words
+            nc.vector.tensor_copy(
+                out=ordered[:].rearrange("p (a u q) -> p a u q", u=2, q=P),
+                in_=x_raw[(c, first)][:].rearrange("p (a q u) -> p a u q", u=2, q=P),
+            )
+            by_pass = ordered[:].rearrange("p (j g w) -> p j g w", g=PASSES, w=PAIRS)
+            for j in range(count):
+                for g in range(PASSES):
+                    x_sorted[(c, first + j, g)] = by_pass[:, j, g, :]
 
-        def frame_slice(c, first, a, u):
-            if x_sorted[(c, first)] is None:
-                return x_raw[(c, first)][:, 256 * a + u : 256 * (a + 1) : 2]
-            return x_sorted[(c, first)][:, P * (2 * a + u) : P * (2 * a + u + 1)]
-
-        def turn_frames(key, c, first, parts):
+        def turn_sorted(parts, out):
             bank = next_bank()
-            for i, a in enumerate(parts):
+            for j, pairs in enumerate(parts):
                 for u in range(2):
                     nc.tensor.transpose(
-                        bank[:, P * (2 * i + u) : P * (2 * i + u + 1)],
-                        frame_slice(c, first, a, u),
+                        bank[:, P * (2 * j + u) : P * (2 * j + u + 1)],
+                        pairs[:, P * u : P * (u + 1)],
                         ident[:],
                     )
-            held[key] = bank
+            nc.scalar.copy(
+                out=out.rearrange("p (j m u) -> p j m u", m=P, u=2),
+                in_=bank[:, 0 : PAIRS * len(parts)].rearrange("p (j u m) -> p j m u", m=P, u=2),
+            )
 
-        def codes_of(c):
-            for g in range(K_PASSES):
+        def new_codes(c):
+            for g in range(PASSES):
                 x_codes[(c, g)] = work.tile(
-                    [P, T], U32, name="x_codes", tag="x_codes", bufs=4, align_bytes=64
+                    [P, T], U32, name="x_codes", tag="x_codes", bufs=2 * PASSES, align_bytes=64
                 )
                 x_scales[(c, g)] = work.tile(
-                    [P, T], U8, name="x_scales", tag="x_scales", bufs=4, align_bytes=64
+                    [P, T], U8, name="x_scales", tag="x_scales", bufs=2 * PASSES, align_bytes=64
                 )
 
-        def turn_tile(j):
-            turn_frames(("x", j), 0, j, (0, 1))
-            turned = work.tile([P, BANK], F32, name="x_turned0", tag="x_turned0", bufs=4, align_bytes=64)
-            copy_out("scalar", turned[:], held[("x", j)][:], 2)
-            x_turned[j] = turned
-
-        def quantize_tile(j):
-            for g in range(K_PASSES):
-                nc.vector.quantize_mx(
-                    out=x_codes[(0, g)][:, P * j : P * (j + 1)].bitcast(FP8X4),
-                    scales=x_scales[(0, g)][:, P * j : P * (j + 1)],
-                    in_=x_turned[j][:, 2 * P * g : 2 * P * (g + 1)].bitcast(BF16),
-                )
+        def quantize_frames(c, g, first, last, turned):
+            nc.vector.quantize_mx(
+                out=x_codes[(c, g)][:, P * first : P * last].bitcast(FP8X4),
+                scales=x_scales[(c, g)][:, P * first : P * last],
+                in_=turned.bitcast(BF16),
+            )
 
         def turn_pass(c, g):
             turned = work.tile([P, 2 * T], F32, name="x_turned", tag="x_turned", bufs=3, align_bytes=64)
-            for h in range(2):
-                turn_frames(("x", c, g, h), c, 2 * h, (g, 2 + g))
-                copy_out("scalar", turned[:, BANK * h : BANK * (h + 1)], held[("x", c, g, h)][:], 2)
+            for j in (0, 2):
+                turn_sorted(
+                    [x_sorted[(c, j, g)], x_sorted[(c, j + 1, g)]],
+                    turned[:, PAIRS * j : PAIRS * (j + 2)],
+                )
             x_turned[(c, g)] = turned
 
-        def quantize_pass(c, g):
-            if g == 0:
-                codes_of(c)
-            nc.vector.quantize_mx(
-                out=x_codes[(c, g)][:].bitcast(FP8X4),
-                scales=x_scales[(c, g)][:],
-                in_=x_turned[(c, g)][:].bitcast(BF16),
-            )
+        cols = keep.tile([P, const_rows], F32, name="cols")
+        amp, squares, squares_turned, y_rows = {}, {}, {}, {}
 
-        used = GAIN_ROWS + EQ_ROWS
-        cols = keep.tile([P, used], F32)
-
-        def turn_constants():
-            bank = next_bank()
-            nc.tensor.transpose(bank[:, 0:P], rows_f32[:], ident[:])
-            nc.scalar.copy(out=cols[:], in_=bank[:, 0:used])
-
-        squares, y_rows, y_pairs, y_turned, y_codes, planes = {}, {}, {}, {}, {}, {}
-
-        def multiply_by_frames(c, j):
-            bank = next_bank()
-            for g in range(K_PASSES):
-                nc.tensor.matmul_mx(
-                    out=bank[:],
-                    lhsT=x_codes[(c, g)][:, P * j : P * (j + 1)].bitcast(FP8X4),
-                    lhsT_scale=x_scales[(c, g)][:, P * j : P * (j + 1)],
-                    rhs=c_words[0][:, g, :].bitcast(FP4X4),
-                    rhs_scale=c_scales[:, g, 0:BANK],
-                    start=(g == 0),
-                    stop=(g == K_PASSES - 1),
-                )
-            held[("amp", c, j)] = bank
-
-        amps = {}
-
-        def equalise(c, j):
-            amp = work.tile([P, BANK], F32, name="amp", tag="amp", bufs=4)
-            nc.vector.tensor_tensor(
-                out=amp[:], in0=held[("amp", c, j)][:], in1=eq_rows[:], op=ALU.mult
-            )
-            amps[(c, j)] = amp
-
-        def square_by_frames(c, j):
-            sq = work.tile([P, BANK], F32, name="sq_frames", tag="sq_frames", bufs=4)
-            nc.scalar.activation(out=sq[:], in_=amps[(c, j)][:], func=ACT.Square)
-            squares[(GROUPS * c, j)] = sq
-
-        def multiply_by_bins(s, b):
+        def multiply(s, b, g):
             c, grp = divmod(s, GROUPS)
-            blk = 4 * grp + b
-            bank = next_bank()
-            for g in range(K_PASSES):
-                nc.tensor.matmul_mx(
-                    out=bank[:],
-                    lhsT=c_words[grp][:, g, 2 * P * b : 2 * P * (b + 1)].bitcast(FP4X4),
-                    lhsT_scale=c_scales[:, g, P * blk : P * (blk + 1)],
-                    rhs=x_codes[(c, g)][:].bitcast(FP8X4),
-                    rhs_scale=x_scales[(c, g)][:],
-                    start=(g == 0),
-                    stop=(g == K_PASSES - 1),
-                )
-            held[("bins", s, b)] = bank
-
-        def square_by_bins(s, b):
-            sq = work.tile([P, T], F32, name="sq_bins", tag="sq_bins", bufs=8)
-            col = GAIN_ROWS + 4 * (s % GROUPS) + b
-            nc.scalar.activation(
-                out=sq[:], in_=held[("bins", s, b)][:], func=ACT.Square, scale=cols[:, col : col + 1]
+            if g == 0:
+                amp[(s, b)] = next_bank()
+            first_bin = BANK * grp + P * b
+            nc.tensor.matmul_mx(
+                out=amp[(s, b)][:],
+                lhsT=c_words[grp][:, g, 2 * P * b : 2 * P * (b + 1)].bitcast(FP4X4),
+                lhsT_scale=c_scales[:, g, first_bin : first_bin + P],
+                rhs=x_codes[(c, g)][:].bitcast(FP8X4),
+                rhs_scale=x_scales[(c, g)][:],
+                start=(g == 0),
+                stop=(g == PASSES - 1),
             )
-            squares[(s, b)] = sq
+            if g == PASSES - 1:
+                sq = work.tile([P, T], F32, name="squares", tag="squares", bufs=2 * BLOCKS)
+                col = GAIN_ROWS + first_bin // P
+                nc.scalar.activation(
+                    out=sq[:], in_=amp[(s, b)][:], func=ACT.Square, scale=cols[:, col : col + 1]
+                )
+                squares[(s, b)] = sq
 
         def turn_squares(s, j, blocks):
             if blocks[0] == 0:
-                held[("sq", s, j)] = next_bank()
-            bank = held[("sq", s, j)]
+                squares_turned[(s, j)] = next_bank()
             for b in blocks:
                 nc.tensor.transpose(
-                    bank[:, P * b : P * (b + 1)], squares[(s, b)][:, P * j : P * (j + 1)], ident[:]
+                    squares_turned[(s, j)][:, P * b : P * (b + 1)],
+                    squares[(s, b)][:, P * j : P * (j + 1)],
+                    ident[:],
                 )
 
         def power(s, j):
             c, grp = divmod(s, GROUPS)
             if j == 0:
-                y_rows[s] = work.tile([P, 4 * BANK], F32, name="y_rows", tag="y_rows", bufs=4)
-            y = y_rows[s]
-            src = squares[(s, j)] if s in TOK else held[("sq", s, j)]
+                y_rows[s] = work.tile([P, TILES * BANK], F32, name="y_rows", tag="y_rows", bufs=4)
+            col = TILES * c + j
             nc.vector.scalar_tensor_tensor(
-                out=y[:, BANK * j : BANK * (j + 1)],
-                in0=src[:],
-                scalar=cols[:, 4 * c + j : 4 * c + j + 1],
-                in1=base_rows[grp],
+                out=y_rows[s][:, BANK * j : BANK * (j + 1)],
+                in0=squares_turned[(s, j)][:],
+                scalar=cols[:, col : col + 1],
+                in1=base_rows[:, BANK * grp : BANK * (grp + 1)],
                 op0=ALU.mult,
                 op1=ALU.add,
             )
             if j % 2 == 1:
                 dst = out_0[c, P * (j - 1) : P * (j + 1), BANK * grp : BANK * (grp + 1)]
+                src = y_rows[s][:, BANK * (j - 1) : BANK * (j + 1)]
                 nc.sync.dma_start(
                     out=dst.rearrange("(j p) n -> p j n", p=P),
-                    in_=y[:, BANK * (j - 1) : BANK * (j + 1)].rearrange("p (j n) -> p j n", j=2),
+                    in_=src.rearrange("p (j n) -> p j n", j=2),
                 )
 
-        def round_pairs(s, j, n, engine):
-            pairs = work.tile([P, n * BANK], BF16, name="y_pairs", tag="y_pairs", bufs=9)
-            src = y_rows[s][:, BANK * j : BANK * (j + n)]
-            copy_on(
-                engine,
-                pairs[:].rearrange("p (j u q e) -> p j u q e", j=n, u=2, e=2),
-                src.rearrange("p (j q u e) -> p j u q e", j=n, u=2, e=2),
-            )
-            for i in range(n):
-                y_pairs[(s, j + i)] = pairs[:, BANK * i : BANK * (i + 1)].bitcast(F32)
+        y_sorted, y_turned, y_codes, y_scales = {}, {}, {}, {}
 
-        def turn_pairs(s, j, n):
-            bank = next_bank()
-            for i in range(n):
-                for u in range(2):
-                    nc.tensor.transpose(
-                        bank[:, P * (2 * i + u) : P * (2 * i + u + 1)],
-                        y_pairs[(s, j + i)][:, P * u : P * (u + 1)],
-                        ident[:],
-                    )
-            held[("y", s, j)] = bank
+        def round_power(s, first, last, engine):
+            count = last - first
+            rounded = work.tile([P, count * BANK], BF16, name="y_sorted", tag="y_sorted", bufs=9)
+            dst = rounded[:].rearrange("p (j u q e) -> p j u q e", u=2, q=P, e=2)
+            src = y_rows[s][:, BANK * first : BANK * last]
+            src = src.rearrange("p (j q u e) -> p j u q e", u=2, q=P, e=2)
+            if engine == "gpsimd":
+                nc.gpsimd.tensor_scalar(
+                    out=dst[:, 0], in0=src[:, 0], scalar1=1.0, scalar2=0.0, op0=ALU.mult, op1=ALU.add
+                )
+            elif engine == "scalar":
+                nc.scalar.copy(out=dst, in_=src)
+            else:
+                nc.vector.tensor_copy(out=dst, in_=src)
+            for j in range(count):
+                y_sorted[(s, first + j)] = rounded[:, BANK * j : BANK * (j + 1)].bitcast(F32)
 
-        def copy_pairs(s, j, n, engine="scalar"):
-            if j == 0:
+        def turn_power(s, first, last):
+            if first == 0:
                 y_turned[s] = work.tile(
                     [P, 2 * T], F32, name="y_turned", tag="y_turned", bufs=4, align_bytes=64
                 )
-            copy_out(
-                engine,
-                y_turned[s][:, 2 * P * j : 2 * P * (j + n)],
-                held[("y", s, j)][:, 0 : 2 * P * n],
-                n,
+            turn_sorted(
+                [y_sorted[(s, j)] for j in range(first, last)],
+                y_turned[s][:, PAIRS * first : PAIRS * last],
             )
 
-        def store_codes(s, first, last):
-            c, grp = divmod(s, GROUPS)
-            dst = out_1[grp, :, T * c + first : T * c + last, :].rearrange("p m t -> p (m t)")
-            nc.sync.dma_start(out=dst.bitcast(I32), in_=y_codes[s][:, first:last].bitcast(I32))
+        def turn_power_halves(s):
+            turn_power(s, 0, 2)
+            turn_power(s, 2, TILES)
 
-        done = {}
-
-        def quantize_power(s, j, n):
+        def quantize_power(s, first, last):
             c, grp = divmod(s, GROUPS)
-            if c not in planes:
-                planes[c] = work.tile(
-                    [P, GROUPS, T], U8, name="y_scales", tag="y_scales", bufs=2, align_bytes=64
-                )
-            if j == 0:
+            if first == 0:
+                if grp == 0:
+                    y_scales[c] = work.tile(
+                        [P, GROUPS, T], U8, name="y_scales", tag="y_scales", bufs=2, align_bytes=64
+                    )
                 y_codes[s] = work.tile(
                     [P, T], U32, name="y_codes", tag="y_codes", bufs=4, align_bytes=64
                 )
             nc.vector.quantize_mx(
-                out=y_codes[s][:, P * j : P * (j + n)].bitcast(FP8X4),
-                scales=planes[c][:, grp, P * j : P * (j + n)],
-                in_=y_turned[s][:, 2 * P * j : 2 * P * (j + n)].bitcast(BF16),
+                out=y_codes[s][:, P * first : P * last].bitcast(FP8X4),
+                scales=y_scales[c][:, grp, P * first : P * last],
+                in_=y_turned[s][:, PAIRS * first : PAIRS * last].bitcast(BF16),
             )
-            if s == UNITS - 1 and j + n >= 3:
-                store_codes(s, 0 if j + n == 3 else 3 * P, P * (j + n))
-            elif j + n == 4:
-                store_codes(s, 0, T)
-            done[c] = done.get(c, 0) + n
-            if done[c] == 4 * GROUPS:
-                for q in range(4):
-                    rows = out_2[:, 4 * q : 4 * q + 4, T * c : T * (c + 1)]
-                    queue = nc.scalar if c == CLIPS - 1 and q < QS else nc.sync
-                    queue.dma_start(
-                        out=rows.rearrange("g r m -> r g m").bitcast(I32),
-                        in_=planes[c][32 * q : 32 * q + 4, :, :].bitcast(I32),
-                    )
 
-        codes_of(0)
-        for j in range(4):
-            sort_frames(0, j, 1)
-            turn_tile(j)
-        for j in range(4):
-            quantize_tile(j)
-            if TOK:
-                multiply_by_frames(0, j)
-        nc.scalar.copy(out=rows_f32[0:used, :], in_=rows_bf[0:used, :])
-        if TOK:
-            equalise(0, 0)
-            square_by_frames(0, 0)
-        turn_constants()
-        if TOK:
-            for j in range(1, 4):
-                equalise(0, j)
-                if j < SQ0:
-                    square_by_frames(0, j)
-        sort_frames(1, 0, 2)
-        sort_frames(1, 2, 2)
-
-        last = UNITS - 1
-        first = len(TOK)
-        for s in range(first, UNITS):
+        def store_codes(s, first, last):
             c, grp = divmod(s, GROUPS)
-            if c == 0 and TOK:
-                passes = (0, 1) if s == 1 else ()
-            else:
-                passes = (grp,) if c + 1 < CLIPS and grp < 2 else ()
-            for b in range(4):
-                multiply_by_bins(s, b)
-                square_by_bins(s, b)
-            if s == 1 and TOK:
-                for j in range(SQ0, 4):
-                    square_by_frames(0, j)
-                power(0, 0)
-                power(0, 1)
-            elif s >= 1:
-                if s in SC and GT == 0:
-                    round_pairs(s - 1, 0, 2, "vector")
-                    round_pairs(s - 1, 2, 2, "scalar")
-                else:
-                    round_pairs(s - 1, GT, 4 - GT, "vector")
+            dst = out_1[grp, :, T * c + P * first : T * c + P * last, :]
+            nc.sync.dma_start(
+                out=dst.rearrange("p m t -> p (m t)").bitcast(I32),
+                in_=y_codes[s][:, P * first : P * last].bitcast(I32),
+            )
+
+        def store_scales(c, queues):
+            for quad in range(QUADRANTS):
+                dst = out_2[:, 4 * quad : 4 * quad + 4, T * c : T * (c + 1)]
+                queues[quad].dma_start(
+                    out=dst.rearrange("grp r m -> r grp m").bitcast(I32),
+                    in_=y_scales[c][32 * quad : 32 * quad + 4, :, :].bitcast(I32),
+                )
+
+        def finish_planes(s):
+            quantize_power(s, 0, TILES)
+            store_codes(s, 0, TILES)
+            if s % GROUPS == GROUPS - 1:
+                store_scales(s // GROUPS, [nc.sync] * QUADRANTS)
+
+        new_codes(0)
+        first_tiles = []
+        for j in range(TILES):
+            sort_frames(0, j, 1)
+            turned = work.tile(
+                [P, PASSES * PAIRS], F32, name="x_first", tag="x_first", bufs=TILES, align_bytes=64
+            )
+            turn_sorted([x_sorted[(0, j, g)] for g in range(PASSES)], turned[:])
+            first_tiles.append(turned)
+        for j in range(TILES):
+            for g in range(PASSES):
+                turned = first_tiles[j][:, PAIRS * g : PAIRS * (g + 1)]
+                quantize_frames(0, g, j, j + 1, turned)
+        nc.scalar.copy(out=rows_f32[0:const_rows, :], in_=rows_bf16[0:const_rows, :])
+        const_bank = next_bank()
+        nc.tensor.transpose(const_bank[:, 0:P], rows_f32[:], ident[:])
+        nc.scalar.copy(out=cols[:], in_=const_bank[:, 0:const_rows])
+        for j in (0, 2):
+            sort_frames(1, j, 2)
+
+        last_unit = UNITS - 1
+        for s in range(UNITS):
+            c, grp = divmod(s, GROUPS)
+            feeds = c + 1 < CLIPS and grp < PASSES
+            for b in range(BLOCKS):
+                for g in range(PASSES):
+                    multiply(s, b, g)
+            if s >= 1:
+                round_power(s - 1, GPSIMD_TILES, TILES, "vector")
             if s >= 3:
-                quantize_power(s - 3, 0, 4)
-            for g in passes:
-                turn_pass(c + 1, g)
-            if grp == 2 and c + 2 < CLIPS:
-                sort_frames(c + 2, 0, 2)
-                sort_frames(c + 2, 2, 2)
-            if s >= 2:
+                finish_planes(s - 3)
+            if feeds:
+                turn_pass(c + 1, grp)
+            elif c + 2 < CLIPS:
                 for j in (0, 2):
-                    turn_pairs(s - 1 if s == last else s - 2, j, 2)
-                    copy_pairs(s - 1 if s == last else s - 2, j, 2)
-            if s == last:
-                quantize_power(s - 2, 0, 4)
-            for j in range(NP):
-                turn_squares(s, j, (0, 1, 2))
-            for j in range(4):
-                turn_squares(s, j, (3,) if j < NP else (0, 1, 2, 3))
+                    sort_frames(c + 2, j, 2)
+            if s == last_unit:
+                turn_power_halves(s - 1)
+                finish_planes(s - 2)
+            elif s >= 2:
+                turn_power_halves(s - 2)
+            for j in range(EARLY_TILES):
+                turn_squares(s, j, range(BLOCKS - 1))
+            for j in range(TILES):
+                turn_squares(s, j, range(BLOCKS - 1 if j < EARLY_TILES else 0, BLOCKS))
                 power(s, j)
-                if s == last:
-                    round_pairs(s, j, 1, "gpsimd" if j < TAILG else "scalar" if j < 3 else "vector")
-                elif j < GT:
-                    round_pairs(s, j, 1, "gpsimd")
-            if s == 1 and TOK:
-                power(0, 2)
-                power(0, 3)
-                round_pairs(0, 0, 4, "vector")
-            if s == last - 1:
-                for j in (0, 2):
-                    turn_pairs(s - 1, j, 2)
-                    copy_pairs(s - 1, j, 2)
-            for g in passes:
-                quantize_pass(c + 1, g)
-        turn_pairs(s, 0, 2)
-        turn_pairs(s, 2, 1)
-        turn_pairs(s, 3, 1)
-        copy_pairs(s, 0, 2)
-        copy_pairs(s, 2, 1, T11)
-        copy_pairs(s, 3, 1)
-        quantize_power(s - 1, 0, 4)
-        quantize_power(s, 0, 2)
-        quantize_power(s, 2, 1)
-        quantize_power(s, 3, 1)
+                if s == last_unit:
+                    round_power(s, j, j + 1, LAST_UNIT_ROUNDERS[j])
+                elif j < GPSIMD_TILES:
+                    round_power(s, j, j + 1, "gpsimd")
+            if s == last_unit - 1:
+                turn_power_halves(s - 1)
+            if feeds:
+                if grp == 0:
+                    new_codes(c + 1)
+                quantize_frames(c + 1, grp, 0, TILES, x_turned[(c + 1, grp)][:])
+
+        pieces = ((0, 2), (2, 3), (3, TILES))
+        for first, last in pieces:
+            turn_power(last_unit, first, last)
+        finish_planes(last_unit - 1)
+        for first, last in pieces:
+            quantize_power(last_unit, first, last)
+            if first > 0:
+                store_codes(last_unit, 0 if last < TILES else first, last)
+        store_scales(CLIPS - 1, [nc.scalar, nc.scalar, nc.sync, nc.sync])

from contextlib import ExitStack

import concourse.mybir as mybir
from concourse.masks import make_identity

CLIPS, T, K, BINS = 4, 512, 1024, 1536
FLOPS = 2 * CLIPS * T * K * BINS

F32 = mybir.dt.float32
BF16 = mybir.dt.bfloat16
I32 = mybir.dt.int32
U32 = mybir.dt.uint32
U8 = mybir.dt.uint8
FP8X4 = mybir.dt.float8_e4m3fn_x4
FP4X4 = mybir.dt.float4_e2m1fn_x4
ALU = mybir.AluOpType
ACT = mybir.ActivationFunctionType

P = 128
BANK = 512
BANKS = 8
PASSES = K // 512
PAIRS = 256
TILES = T // P
BLOCKS = BANK // P
GROUPS = BINS // BANK
UNITS = CLIPS * GROUPS
QUADRANTS = 4
X_LOADS = TILES + (CLIPS - 1) * TILES // 2
GAIN_ROWS = CLIPS * TILES
EQ_ROWS = BINS // P
GPSIMD_TILES = 2
LAST_UNIT_ROUNDERS = ("scalar", "scalar", "scalar", "vector")
EARLY_TILES = 3


def tile_cosine_power_for_mel_g4_kernel(
    tc, frames, basis_words, basis_scales, eq, frame_gain, base_power, out_0, out_1, out_2
):
    nc = tc.nc
    with ExitStack() as ctx:
        keep = ctx.enter_context(tc.tile_pool(name="keep", bufs=1))
        work = ctx.enter_context(tc.tile_pool(name="work", bufs=1))
        psum = ctx.enter_context(tc.psum_pool(name="psum", bufs=1))
        ctx.enter_context(tc.manual_schedule())

        banks_taken = []

        def next_bank():
            tag = "bank%d" % (len(banks_taken) % BANKS)
            banks_taken.append(tag)
            return psum.tile([P, BANK], F32, name=tag, tag=tag)

        ident = keep.tile([P, P], F32, name="ident")
        make_identity(nc, ident[:])
        rows_f32 = keep.tile([P, P], F32, name="rows_f32")
        c_scales = keep.tile([P, PASSES, BINS], U8, name="c_scales", align_bytes=64)
        nc.vector.memset(c_scales[:].rearrange("p g n -> p (g n)").bitcast(I32), 0)
        nc.vector.memset(rows_f32[:], 0.0)
        rows_bf16 = keep.tile([P, P], BF16, name="rows_bf16")

        frame_pairs = frames.bitcast(F32)
        x_raw, x_sorted, c_words = {}, {}, {}

        def load_frames(c, first, count):
            raw = work.tile([P, count * PASSES * PAIRS], F32, name="x_raw", tag="x_raw", bufs=X_LOADS)
            src = frame_pairs[c, P * first : P * (first + count), :]
            nc.sync.dma_start(
                out=raw[:].rearrange("p (j w) -> p j w", j=count),
                in_=src.rearrange("(j p) w -> p j w", p=P),
            )
            x_raw[(c, first)] = raw

        def load_basis(grp):
            words = keep.tile([P, PASSES, 2 * BANK], U8, name="c_words%d" % grp, align_bytes=64)
            src = basis_words[:, :, 2 * BANK * grp : 2 * BANK * (grp + 1)]
            nc.sync.dma_start(
                out=words[:].bitcast(I32), in_=src.rearrange("g p n -> p g n").bitcast(I32)
            )
            c_words[grp] = words

        for j in range(TILES):
            load_frames(0, j, 1)
        for quad in range(QUADRANTS):
            src = basis_scales[:, 4 * quad : 4 * quad + 4, :].rearrange("g r n -> r g n")
            nc.sync.dma_start(
                out=c_scales[32 * quad : 32 * quad + 4, :, :].bitcast(I32), in_=src.bitcast(I32)
            )
        load_basis(0)
        const_rows = GAIN_ROWS + EQ_ROWS
        nc.sync.dma_start(
            out=rows_bf16[0:GAIN_ROWS, :], in_=frame_gain.rearrange("c (j p) -> (c j) p", p=P)
        )
        nc.sync.dma_start(
            out=rows_bf16[GAIN_ROWS:const_rows, :], in_=eq.rearrange("(b p) -> b p", p=P)
        )
        for j in (0, 2):
            load_frames(1, j, 2)
        load_basis(1)
        base_rows = keep.tile([P, BINS], BF16, name="base_rows")
        nc.sync.dma_start(out=base_rows[:], in_=base_power.partition_broadcast(P))
        load_basis(2)
        for c in range(2, CLIPS):
            for j in (0, 2):
                load_frames(c, j, 2)

        x_turned, x_codes, x_scales = {}, {}, {}

        def sort_frames(c, first, count):
            ordered = work.tile(
                [P, count * PASSES * PAIRS], F32, name="x_sorted", tag="x_sorted", bufs=4
            )
            nc.vector.tensor_copy(
                out=ordered[:].rearrange("p (a u q) -> p a u q", u=2, q=P),
                in_=x_raw[(c, first)][:].rearrange("p (a q u) -> p a u q", u=2, q=P),
            )
            by_pass = ordered[:].rearrange("p (j g w) -> p j g w", g=PASSES, w=PAIRS)
            for j in range(count):
                for g in range(PASSES):
                    x_sorted[(c, first + j, g)] = by_pass[:, j, g, :]

        def turn_sorted(parts, out):
            bank = next_bank()
            for j, pairs in enumerate(parts):
                for u in range(2):
                    nc.tensor.transpose(
                        bank[:, P * (2 * j + u) : P * (2 * j + u + 1)],
                        pairs[:, P * u : P * (u + 1)],
                        ident[:],
                    )
            nc.scalar.copy(
                out=out.rearrange("p (j m u) -> p j m u", m=P, u=2),
                in_=bank[:, 0 : PAIRS * len(parts)].rearrange("p (j u m) -> p j m u", m=P, u=2),
            )

        def new_codes(c):
            for g in range(PASSES):
                x_codes[(c, g)] = work.tile(
                    [P, T], U32, name="x_codes", tag="x_codes", bufs=2 * PASSES, align_bytes=64
                )
                x_scales[(c, g)] = work.tile(
                    [P, T], U8, name="x_scales", tag="x_scales", bufs=2 * PASSES, align_bytes=64
                )

        def quantize_frames(c, g, first, last, turned):
            nc.vector.quantize_mx(
                out=x_codes[(c, g)][:, P * first : P * last].bitcast(FP8X4),
                scales=x_scales[(c, g)][:, P * first : P * last],
                in_=turned.bitcast(BF16),
            )

        def turn_pass(c, g):
            turned = work.tile([P, 2 * T], F32, name="x_turned", tag="x_turned", bufs=3, align_bytes=64)
            for j in (0, 2):
                turn_sorted(
                    [x_sorted[(c, j, g)], x_sorted[(c, j + 1, g)]],
                    turned[:, PAIRS * j : PAIRS * (j + 2)],
                )
            x_turned[(c, g)] = turned

        cols = keep.tile([P, const_rows], F32, name="cols")
        amp, squares, squares_turned, y_rows = {}, {}, {}, {}

        def multiply(s, b, g):
            c, grp = divmod(s, GROUPS)
            if g == 0:
                amp[(s, b)] = next_bank()
            first_bin = BANK * grp + P * b
            nc.tensor.matmul_mx(
                out=amp[(s, b)][:],
                lhsT=c_words[grp][:, g, 2 * P * b : 2 * P * (b + 1)].bitcast(FP4X4),
                lhsT_scale=c_scales[:, g, first_bin : first_bin + P],
                rhs=x_codes[(c, g)][:].bitcast(FP8X4),
                rhs_scale=x_scales[(c, g)][:],
                start=(g == 0),
                stop=(g == PASSES - 1),
            )
            if g == PASSES - 1:
                sq = work.tile([P, T], F32, name="squares", tag="squares", bufs=2 * BLOCKS)
                col = GAIN_ROWS + first_bin // P
                nc.scalar.activation(
                    out=sq[:], in_=amp[(s, b)][:], func=ACT.Square, scale=cols[:, col : col + 1]
                )
                squares[(s, b)] = sq

        def turn_squares(s, j, blocks):
            if blocks[0] == 0:
                squares_turned[(s, j)] = next_bank()
            for b in blocks:
                nc.tensor.transpose(
                    squares_turned[(s, j)][:, P * b : P * (b + 1)],
                    squares[(s, b)][:, P * j : P * (j + 1)],
                    ident[:],
                )

        def power(s, j):
            c, grp = divmod(s, GROUPS)
            if j == 0:
                y_rows[s] = work.tile([P, TILES * BANK], F32, name="y_rows", tag="y_rows", bufs=4)
            col = TILES * c + j
            nc.vector.scalar_tensor_tensor(
                out=y_rows[s][:, BANK * j : BANK * (j + 1)],
                in0=squares_turned[(s, j)][:],
                scalar=cols[:, col : col + 1],
                in1=base_rows[:, BANK * grp : BANK * (grp + 1)],
                op0=ALU.mult,
                op1=ALU.add,
            )
            if j % 2 == 1:
                dst = out_0[c, P * (j - 1) : P * (j + 1), BANK * grp : BANK * (grp + 1)]
                src = y_rows[s][:, BANK * (j - 1) : BANK * (j + 1)]
                nc.sync.dma_start(
                    out=dst.rearrange("(j p) n -> p j n", p=P),
                    in_=src.rearrange("p (j n) -> p j n", j=2),
                )

        y_sorted, y_turned, y_codes, y_scales = {}, {}, {}, {}

        def round_power(s, first, last, engine):
            count = last - first
            rounded = work.tile([P, count * BANK], BF16, name="y_sorted", tag="y_sorted", bufs=9)
            dst = rounded[:].rearrange("p (j u q e) -> p j u q e", u=2, q=P, e=2)
            src = y_rows[s][:, BANK * first : BANK * last]
            src = src.rearrange("p (j q u e) -> p j u q e", u=2, q=P, e=2)
            if engine == "gpsimd":
                nc.gpsimd.tensor_scalar(
                    out=dst[:, 0], in0=src[:, 0], scalar1=1.0, scalar2=0.0, op0=ALU.mult, op1=ALU.add
                )
            elif engine == "scalar":
                nc.scalar.copy(out=dst, in_=src)
            else:
                nc.vector.tensor_copy(out=dst, in_=src)
            for j in range(count):
                y_sorted[(s, first + j)] = rounded[:, BANK * j : BANK * (j + 1)].bitcast(F32)

        def turn_power(s, first, last):
            if first == 0:
                y_turned[s] = work.tile(
                    [P, 2 * T], F32, name="y_turned", tag="y_turned", bufs=4, align_bytes=64
                )
            turn_sorted(
                [y_sorted[(s, j)] for j in range(first, last)],
                y_turned[s][:, PAIRS * first : PAIRS * last],
            )

        def turn_power_halves(s):
            turn_power(s, 0, 2)
            turn_power(s, 2, TILES)

        def quantize_power(s, first, last):
            c, grp = divmod(s, GROUPS)
            if first == 0:
                if grp == 0:
                    y_scales[c] = work.tile(
                        [P, GROUPS, T], U8, name="y_scales", tag="y_scales", bufs=2, align_bytes=64
                    )
                y_codes[s] = work.tile(
                    [P, T], U32, name="y_codes", tag="y_codes", bufs=4, align_bytes=64
                )
            nc.vector.quantize_mx(
                out=y_codes[s][:, P * first : P * last].bitcast(FP8X4),
                scales=y_scales[c][:, grp, P * first : P * last],
                in_=y_turned[s][:, PAIRS * first : PAIRS * last].bitcast(BF16),
            )

        def store_codes(s, first, last):
            c, grp = divmod(s, GROUPS)
            dst = out_1[grp, :, T * c + P * first : T * c + P * last, :]
            nc.sync.dma_start(
                out=dst.rearrange("p m t -> p (m t)").bitcast(I32),
                in_=y_codes[s][:, P * first : P * last].bitcast(I32),
            )

        def store_scales(c, queues):
            for quad in range(QUADRANTS):
                dst = out_2[:, 4 * quad : 4 * quad + 4, T * c : T * (c + 1)]
                queues[quad].dma_start(
                    out=dst.rearrange("grp r m -> r grp m").bitcast(I32),
                    in_=y_scales[c][32 * quad : 32 * quad + 4, :, :].bitcast(I32),
                )

        def finish_planes(s):
            quantize_power(s, 0, TILES)
            store_codes(s, 0, TILES)
            if s % GROUPS == GROUPS - 1:
                store_scales(s // GROUPS, [nc.sync] * QUADRANTS)

        new_codes(0)
        first_tiles = []
        for j in range(TILES):
            sort_frames(0, j, 1)
            turned = work.tile(
                [P, PASSES * PAIRS], F32, name="x_first", tag="x_first", bufs=TILES, align_bytes=64
            )
            turn_sorted([x_sorted[(0, j, g)] for g in range(PASSES)], turned[:])
            first_tiles.append(turned)
        for j in range(TILES):
            for g in range(PASSES):
                turned = first_tiles[j][:, PAIRS * g : PAIRS * (g + 1)]
                quantize_frames(0, g, j, j + 1, turned)
        nc.scalar.copy(out=rows_f32[0:const_rows, :], in_=rows_bf16[0:const_rows, :])
        const_bank = next_bank()
        nc.tensor.transpose(const_bank[:, 0:P], rows_f32[:], ident[:])
        nc.scalar.copy(out=cols[:], in_=const_bank[:, 0:const_rows])
        for j in (0, 2):
            sort_frames(1, j, 2)

        last_unit = UNITS - 1
        for s in range(UNITS):
            c, grp = divmod(s, GROUPS)
            feeds = c + 1 < CLIPS and grp < PASSES
            for b in range(BLOCKS):
                for g in range(PASSES):
                    multiply(s, b, g)
            if s >= 1:
                round_power(s - 1, GPSIMD_TILES, TILES, "vector")
            if s >= 3:
                finish_planes(s - 3)
            if feeds:
                turn_pass(c + 1, grp)
            elif c + 2 < CLIPS:
                for j in (0, 2):
                    sort_frames(c + 2, j, 2)
            if s == last_unit:
                turn_power_halves(s - 1)
                finish_planes(s - 2)
            elif s >= 2:
                turn_power_halves(s - 2)
            for j in range(EARLY_TILES):
                turn_squares(s, j, range(BLOCKS - 1))
            for j in range(TILES):
                turn_squares(s, j, range(BLOCKS - 1 if j < EARLY_TILES else 0, BLOCKS))
                power(s, j)
                if s == last_unit:
                    round_power(s, j, j + 1, LAST_UNIT_ROUNDERS[j])
                elif j < GPSIMD_TILES:
                    round_power(s, j, j + 1, "gpsimd")
            if s == last_unit - 1:
                turn_power_halves(s - 1)
            if feeds:
                if grp == 0:
                    new_codes(c + 1)
                quantize_frames(c + 1, grp, 0, TILES, x_turned[(c + 1, grp)][:])

        pieces = ((0, 2), (2, 3), (3, TILES))
        for first, last in pieces:
            turn_power(last_unit, first, last)
        finish_planes(last_unit - 1)
        for first, last in pieces:
            quantize_power(last_unit, first, last)
            if first > 0:
                store_codes(last_unit, 0 if last < TILES else first, last)
        store_scales(CLIPS - 1, [nc.scalar, nc.scalar, nc.sync, nc.sync])
